import numpy as np
import ml_dtypes


def mxq(x, axis, fmt="e4m3"):
    dtype, down = {"e4m3": (ml_dtypes.float8_e4m3fn, 7), "e5m2": (ml_dtypes.float8_e5m2, 14)}[fmt]
    v = np.moveaxis(np.asarray(x, np.float32).astype(ml_dtypes.bfloat16).astype(np.float64), axis, -1)
    blocks = v.reshape(v.shape[:-1] + (-1, 32))
    amax = np.abs(blocks).max(-1, keepdims=True)
    byte = np.maximum(np.where(amax > 0, np.frexp(amax)[1] - 1 + 127, 0) - down, 1)
    scale = np.exp2(byte - 127.0)
    codes = (blocks / scale).astype(np.float32).astype(dtype).astype(np.float64)
    return np.moveaxis((codes * scale).reshape(v.shape), -1, axis)


WIDE = False


def mx_kscale(k):
    if not WIDE:
        return np.ones(k)
    levels = np.array([10, -10, 5, -5, 0])
    if k % 512:
        return np.exp2(np.random.permutation(np.resize(levels, k // 32))).repeat(32)
    a = np.empty((k // 512, 16))
    for p in range(k // 512):
        a[p, :8] = np.random.permutation(np.resize(levels, 8))
        for g in range(8):
            far = levels[np.abs(levels - a[p, g]) >= 10]
            a[p, g + 8] = far[np.random.randint(len(far))]
    return np.exp2(a.ravel()).repeat(32)


def f64(x):
    return np.asarray(x).astype(np.float64)


def striped(idx):
    return np.tile(idx.reshape(-1, 16).T, (8, 1)).astype(np.uint16)


def unstriped(offs):
    return offs[:16].T.reshape(-1).astype(np.int64)


E2M1 = np.array([0.0, 0.5, 1.0, 1.5, 2.0, 3.0, 4.0, 6.0, -0.0, -0.5, -1.0, -1.5, -2.0, -3.0, -4.0, -6.0])


def pack_weight(w, fmt):
    k, n = w.shape
    w = f64(np.asarray(w, np.float32).astype(ml_dtypes.bfloat16)).reshape(k // 32, 32, n)
    amax = np.abs(w).max(1)
    if fmt == "e4m3":
        byte = np.frexp(amax)[1] - 1 + 127 - 7
    else:
        mant, ex = np.frexp(amax / 6.0)
        byte = np.where(mant > 0.5, ex, ex - 1) + 127
    byte = np.clip(np.where(amax > 0, byte, 1), 1, 254)
    scaled = (w * np.exp2(127.0 - byte)[:, None, :]).reshape(k, n).astype(np.float32)
    by_word = np.ascontiguousarray(scaled.reshape(k // 512, 128, 4, n).transpose(0, 1, 3, 2))
    if fmt == "e4m3":
        words = by_word.astype(ml_dtypes.float8_e4m3fn).view(np.uint8)
    else:
        c = by_word.astype(ml_dtypes.float4_e2m1fn).view(np.uint8) & 0xF
        words = (c[..., 0::2] | (c[..., 1::2] << 4)).reshape(k // 512, 128, 2 * n)
    return np.ascontiguousarray(words), np.ascontiguousarray(byte.astype(np.uint8).reshape(k // 512, 16, n))


def unpack_weight(words, scales, fmt):
    g, _, n = scales.shape
    words = np.ascontiguousarray(words).reshape(g, 128, n, -1)
    if fmt == "e4m3":
        vals = words.view(ml_dtypes.float8_e4m3fn).astype(np.float64)
    else:
        nib = np.empty((g, 128, n, 4), np.uint8)
        nib[..., 0::2] = words & 0xF
        nib[..., 1::2] = words >> 4
        vals = E2M1[nib]
    vals = vals * np.repeat(np.exp2(scales.astype(np.float64) - 127.0), 8, axis=1)[..., None]
    return vals.transpose(0, 1, 3, 2).reshape(g * 512, n)


def relu2(v):
    return np.maximum(v, 0.0) ** 2


K, T, E, C, N = 1024, 1024, 8, 128, 512
K8 = 512


def by_expert(wq, xq):
    return np.concatenate([wq[e].T @ xq[:, e * C:(e + 1) * C] for e in range(E)], axis=1)


def setup_inputs():
    n = np.random.standard_normal
    s = mx_kscale(K)[:, None]
    w = n((E, K, N)) / np.sqrt(K) / s[None]
    w8 = [pack_weight(m[:K8], "e4m3") for m in w]
    w4 = [pack_weight(m[K8:], "e2m1") for m in w]
    return {
        "xT": (n((K, T)) * s).astype(np.float32),
        "w8_words": np.stack([m[0] for m in w8]),
        "w8_scales": np.stack([m[1] for m in w8]),
        "w4_words": np.stack([m[0] for m in w4]),
        "w4_scales": np.stack([m[1] for m in w4]),
        "b": (0.3 * n((N, E))).astype(np.float32),
        "gate": np.tile(np.random.uniform(0.2, 1.0, E * C), (N, 1)).astype(np.float32),
        "offs": striped(np.random.permutation(T)[:E * C]),
        "dst": striped(np.random.permutation(T)[:E * C]),
    }


def reference(xT, w8_words, w8_scales, w4_words, w4_scales, b, gate, offs, dst):
    idx = unstriped(offs)
    w = np.stack([np.concatenate([unpack_weight(w8_words[e], w8_scales[e], "e4m3"), unpack_weight(w4_words[e], w4_scales[e], "e2m1")]) for e in range(E)])
    xq = mxq(f64(xT)[:, idx], 0, "e4m3")
    y = by_expert(w, xq)
    y = relu2(y + np.repeat(f64(b), C, axis=1))
    out = np.zeros((N, T))
    out[:, unstriped(dst)] = f64(gate) * y
    return out

@@ -1,0 +1,174 @@
+import concourse.mybir as mybir
+
+K, T, E, C, N = 1024, 1024, 8, 128, 512
+P = 128
+J = 4
+FLOPS = 2 * K * N * E * C
+BYTES = K * T * 4 + E * 128 * 512 * 6 + 2 * E * 16 * 512 + N * E * 4 + T * 4 + 2 * P * 64 * 2 + N * T * 4
+
+F32 = mybir.dt.float32
+BF16 = mybir.dt.bfloat16
+U32 = mybir.dt.uint32
+I32 = mybir.dt.int32
+U16 = mybir.dt.uint16
+U8 = mybir.dt.uint8
+FP8X4 = mybir.dt.float8_e4m3fn_x4
+FP4X4 = mybir.dt.float4_e2m1fn_x4
+RELU = mybir.ActivationFunctionType.Relu
+SQUARE = mybir.ActivationFunctionType.Square
+MULT = mybir.AluOpType.mult
+
+NT = N // P
+HALF = T // 2
+CHUNKS = (
+    ((0, 512, 320), (512, 512, 320)),
+    ((0, 512, 160), (512, 256, 128), (768, 256, 160)),
+)
+PLANE = (4, 0)
+PIECES = (
+    (0, 0, 2), (1, 0, 2), (0, 2, 4), (1, 2, 4), (0, 4, 8), (1, 4, 8),
+    (2, 0, 4), (3, 0, 4), (2, 4, 8), (3, 4, 8),
+)
+
+
+def tile_moe_two_lin_relu2_kernel(tc, xT, w8_words, w8_scales, w4_words, w4_scales, b, gate, offs, dst, out):
+    nc = tc.nc
+    with tc.tile_pool(name="keep", bufs=1) as keep, tc.psum_pool(name="psum", bufs=1) as psum:
+        offs_t = keep.tile([P, 64], U16, name="offs_t")
+        dst_t = keep.tile([P, 64], U16, name="dst_t")
+        bias = keep.tile([P, NT, E], F32, name="bias")
+        gate_t = keep.tile([P, T], F32, name="gate_t")
+        words = [keep.tile([P, T], U32, name=f"words{a}", align_bytes=256) for a in range(2)]
+        scales = keep.tile([P, T], U8, name="scales", align_bytes=256)
+        g_words = [keep.tile([P, T], U32, name=f"g_words{a}", align_bytes=256) for a in range(2)]
+        g_scales = keep.tile([P, T], U8, name="g_scales", align_bytes=256)
+        w8_t = keep.tile([P, E, 4 * N], U8, name="w8_t", align_bytes=256)
+        w4_t = keep.tile([P, E, 2 * N], U8, name="w4_t", align_bytes=256)
+        w_sc = keep.tile([P, E * N], U8, name="w_sc", align_bytes=256)
+        window = [keep.tile([P, T], F32, name=f"window{n}") for n in range(NT)]
+        banks = [[psum.tile([P, HALF], F32, name=f"bank{n}_{h}") for h in range(2)] for n in range(NT)]
+
+        nc.gpsimd.memset(scales[:], 0)
+        nc.vector.memset(w_sc[:].bitcast(I32), 0)
+
+        def load_w8(e0, e1):
+            nc.sync.dma_start(
+                out=w8_t[:, e0:e1, :].bitcast(I32),
+                in_=w8_words[e0:e1].rearrange("e a p n r -> (a p) e (n r)").bitcast(I32),
+            )
+
+        def load_w4(e0, e1):
+            nc.sync.dma_start(
+                out=w4_t[:, e0:e1, :].bitcast(I32), in_=w4_words[e0:e1].rearrange("e a p n -> (a p) e n").bitcast(I32)
+            )
+
+        def load_scales(r):
+            for plane, sc in ((0, w4_scales), (4, w8_scales)):
+                nc.sync.dma_start(
+                    out=w_sc[plane + r : P : 32, :].bitcast(I32).rearrange("q (e n) -> q e n", e=E),
+                    in_=sc.bitcast(I32).rearrange("e a (q r) n -> r a q e n", r=4)[r][0],
+                )
+
+        def load_gate(h):
+            nc.sync.dma_start(out=gate_t[:, h * HALF : (h + 1) * HALF], in_=gate[0:P, h * HALF : (h + 1) * HALF])
+
+        x_view = xT.rearrange("(a p j) t -> a p j t", a=2, j=J)
+        raws, grouped = {}, {}
+        for a in range(2):
+            for i, (t0, width, v) in enumerate(CHUNKS[a]):
+                raws[a, i] = keep.tile([P, J, width], F32, name=f"raw{a}_{i}")
+                grouped[a, i] = keep.tile([P, width, J], BF16, name=f"grouped{a}_{i}", align_bytes=256)
+                if (a, i) == (1, 2):
+                    load_scales(0)
+                    load_scales(1)
+                nc.sync.dma_start(out=raws[a, i][:], in_=x_view[a][:, :, t0 : t0 + width])
+                if (a, i) == (0, 0):
+                    nc.sync.dma_start(offs_t[:], offs)
+
+        load_w8(0, 2)
+        load_scales(2)
+        load_scales(3)
+        nc.sync.dma_start(out=bias[:], in_=b.rearrange("(n p) e -> p n e", p=P))
+        load_w4(0, 4)
+        load_w8(2, 4)
+        load_gate(0)
+        nc.sync.dma_start(dst_t[:], dst)
+        load_w8(4, 6)
+        load_w4(4, 8)
+        load_w8(6, 8)
+        load_gate(1)
+
+        def interleave(a, i):
+            t0, width, v = CHUNKS[a][i]
+            for copy, lo, hi in ((nc.vector.tensor_copy, 0, v), (nc.scalar.copy, v, width)):
+                copy(
+                    out=grouped[a, i][:, lo:hi, :].rearrange("p (c i) j -> p c j i", i=4),
+                    in_=raws[a, i][:, :, lo:hi].rearrange("p j (c i) -> p c j i", i=4),
+                )
+
+        def quantise(a, i):
+            t0, width, v = CHUNKS[a][i]
+            nc.vector.quantize_mx(
+                out=words[a][:, t0 : t0 + width].bitcast(FP8X4),
+                scales=scales[PLANE[a] : P, t0 : t0 + width],
+                in_=grouped[a, i][:].rearrange("p t j -> p (t j)"),
+            )
+
+        def gather(to, of, e0, e1):
+            nc.vector.tensor_copy(to[:, e0 * C : e1 * C], of[:].indirect(offs_t[:, 8 * e0 : 8 * e1]))
+
+        interleave(0, 0)
+        interleave(0, 1)
+        quantise(0, 0)
+        quantise(0, 1)
+        gather(g_words[0], words[0], 0, 4)
+        gather(g_words[0], words[0], 4, 8)
+        interleave(1, 0)
+        interleave(1, 1)
+        quantise(1, 0)
+        interleave(1, 2)
+        quantise(1, 1)
+        quantise(1, 2)
+        for e0, e1 in ((0, 2), (2, 4), (4, 8)):
+            gather(g_scales, scales, e0, e1)
+            gather(g_words[1], words[1], e0, e1)
+
+        for n, e0, e1 in PIECES:
+            half = e0 // 4
+            width = (e1 - e0) * C
+            relu = keep.tile([P, width], F32, name=f"relu{n}_{e0}")
+            squared = keep.tile([P, width], F32, name=f"squared{n}_{e0}")
+            bank = banks[n][half]
+            for e in range(e0, e1):
+                place = slice((e - 4 * half) * C, (e - 4 * half + 1) * C)
+                slots = slice(e * C, (e + 1) * C)
+                w_cols = slice(e * N + n * P, e * N + (n + 1) * P)
+                nc.tensor.matmul_mx(
+                    out=bank[:, place],
+                    lhsT=w8_t[:, e, 4 * n * P : 4 * (n + 1) * P].bitcast(FP8X4),
+                    lhsT_scale=w_sc[4:P, w_cols],
+                    rhs=g_words[0][:, slots].bitcast(FP8X4),
+                    rhs_scale=g_scales[4:P, slots],
+                    start=True,
+                    stop=False,
+                )
+                nc.tensor.matmul_mx(
+                    out=bank[:, place],
+                    lhsT=w4_t[:, e, 2 * n * P : 2 * (n + 1) * P].bitcast(FP4X4),
+                    lhsT_scale=w_sc[:, w_cols],
+                    rhs=g_words[1][:, slots].bitcast(FP8X4),
+                    rhs_scale=g_scales[:, slots],
+                    start=False,
+                    stop=True,
+                )
+            for e in range(e0, e1):
+                place = slice((e - 4 * half) * C, (e - 4 * half + 1) * C)
+                nc.scalar.activation(
+                    relu[:, (e - e0) * C : (e - e0 + 1) * C], bank[:, place], RELU, bias=bias[:, n, e : e + 1]
+                )
+            nc.scalar.activation(squared[:], relu[:], SQUARE)
+            nc.vector.tensor_tensor(
+                window[n][:].indirect(dst_t[:, 8 * e0 : 8 * e1]), squared[:], gate_t[:, e0 * C : e1 * C], MULT
+            )
+            if e1 == E:
+                nc.sync.dma_start(out=out[n * P : (n + 1) * P, :], in_=window[n][:])

@@ -26,8 +26,7 @@ CHUNKS = (
 )
 PLANE = (4, 0)
 PIECES = (
-    (0, 0, 2), (1, 0, 2), (0, 2, 4), (1, 2, 4), (0, 4, 8), (1, 4, 8),
-    (2, 0, 4), (3, 0, 4), (2, 4, 8), (3, 4, 8),
+    (0, 0, 2), (1, 0, 2), (0, 2, 4), (1, 2, 4), (0, 4, 8), (1, 4, 8), (2, 0, 8), (3, 0, 8),
 )
 
 
@@ -45,7 +44,7 @@ def tile_moe_two_lin_relu2_kernel(tc, xT, w8_words, w8_scales, w4_words, w4_scal
         w8_t = keep.tile([P, E, 4 * N], U8, name="w8_t", align_bytes=256)
         w4_t = keep.tile([P, E, 2 * N], U8, name="w4_t", align_bytes=256)
         w_sc = keep.tile([P, E * N], U8, name="w_sc", align_bytes=256)
-        window = [keep.tile([P, T], F32, name=f"window{n}") for n in range(NT)]
+        window = [keep.tile([P, T if n < 2 else 2 * T], F32, name=f"window{n}") for n in range(NT)]
         banks = [[psum.tile([P, HALF], F32, name=f"bank{n}_{h}") for h in range(2)] for n in range(NT)]
 
         nc.gpsimd.memset(scales[:], 0)
@@ -129,18 +128,17 @@ def tile_moe_two_lin_relu2_kernel(tc, xT, w8_words, w8_scales, w4_words, w4_scal
         interleave(1, 2)
         quantise(1, 1)
         quantise(1, 2)
-        for e0, e1 in ((0, 2), (2, 4), (4, 8)):
+        for e0, e1 in ((0, 2), (2, 8)):
             gather(g_scales, scales, e0, e1)
             gather(g_words[1], words[1], e0, e1)
 
         for n, e0, e1 in PIECES:
-            half = e0 // 4
             width = (e1 - e0) * C
             relu = keep.tile([P, width], F32, name=f"relu{n}_{e0}")
             squared = keep.tile([P, width], F32, name=f"squared{n}_{e0}")
-            bank = banks[n][half]
             for e in range(e0, e1):
-                place = slice((e - 4 * half) * C, (e - 4 * half + 1) * C)
+                bank = banks[n][e // 4]
+                place = slice(e % 4 * C, (e % 4 + 1) * C)
                 slots = slice(e * C, (e + 1) * C)
                 w_cols = slice(e * N + n * P, e * N + (n + 1) * P)
                 nc.tensor.matmul_mx(
@@ -162,7 +160,8 @@ def tile_moe_two_lin_relu2_kernel(tc, xT, w8_words, w8_scales, w4_words, w4_scal
                     stop=True,
                 )
             for e in range(e0, e1):
-                place = slice((e - 4 * half) * C, (e - 4 * half + 1) * C)
+                bank = banks[n][e // 4]
+                place = slice(e % 4 * C, (e % 4 + 1) * C)
                 nc.scalar.activation(
                     relu[:, (e - e0) * C : (e - e0 + 1) * C], bank[:, place], RELU, bias=bias[:, n, e : e + 1]
                 )
@@ -171,4 +170,4 @@ def tile_moe_two_lin_relu2_kernel(tc, xT, w8_words, w8_scales, w4_words, w4_scal
                 window[n][:].indirect(dst_t[:, 8 * e0 : 8 * e1]), squared[:], gate_t[:, e0 * C : e1 * C], MULT
             )
             if e1 == E:
-                nc.sync.dma_start(out=out[n * P : (n + 1) * P, :], in_=window[n][:])
+                nc.sync.dma_start(out=out[n * P : (n + 1) * P, :], in_=window[n][:, 0:T])

@@ -22,11 +22,11 @@ NT = N // P
 HALF = T // 2
 CHUNKS = (
     ((0, 512, 320), (512, 512, 320)),
-    ((0, 512, 160), (512, 256, 128), (768, 256, 160)),
+    ((0, 256, 0), (256, 256, 0), (512, 256, 96), (768, 256, 160)),
 )
 PLANE = (4, 0)
 PIECES = (
-    (0, 0, 2), (1, 0, 2), (0, 2, 4), (1, 2, 4), (0, 4, 8), (1, 4, 8), (2, 0, 8), (3, 0, 8),
+    (0, 0, 1), (1, 0, 1), (2, 0, 2), (3, 0, 2), (0, 1, 4), (1, 1, 4), (2, 2, 8), (3, 2, 8), (0, 4, 8), (1, 4, 8),
 )
 
 
@@ -37,7 +37,7 @@ def tile_moe_two_lin_relu2_kernel(tc, xT, w8_words, w8_scales, w4_words, w4_scal
         dst_t = keep.tile([P, 64], U16, name="dst_t")
         bias = keep.tile([P, NT, E], F32, name="bias")
         gate_t = keep.tile([P, T], F32, name="gate_t")
-        words = [keep.tile([P, T], U32, name=f"words{a}", align_bytes=256) for a in range(2)]
+        words = [keep.tile([P, 2 * T if a == 0 else T], U32, name=f"words{a}", align_bytes=256) for a in range(2)]
         scales = keep.tile([P, T], U8, name="scales", align_bytes=256)
         g_words = [keep.tile([P, T], U32, name=f"g_words{a}", align_bytes=256) for a in range(2)]
         g_scales = keep.tile([P, T], U8, name="g_scales", align_bytes=256)
@@ -68,8 +68,8 @@ def tile_moe_two_lin_relu2_kernel(tc, xT, w8_words, w8_scales, w4_words, w4_scal
                     in_=sc.bitcast(I32).rearrange("e a (q r) n -> r a q e n", r=4)[r][0],
                 )
 
-        def load_gate(h):
-            nc.sync.dma_start(out=gate_t[:, h * HALF : (h + 1) * HALF], in_=gate[0:P, h * HALF : (h + 1) * HALF])
+        def load_gate(e0, e1):
+            nc.sync.dma_start(out=gate_t[:, e0 * C : e1 * C], in_=gate[0:P, e0 * C : e1 * C])
 
         x_view = xT.rearrange("(a p j) t -> a p j t", a=2, j=J)
         raws, grouped = {}, {}
@@ -77,29 +77,30 @@ def tile_moe_two_lin_relu2_kernel(tc, xT, w8_words, w8_scales, w4_words, w4_scal
             for i, (t0, width, v) in enumerate(CHUNKS[a]):
                 raws[a, i] = keep.tile([P, J, width], F32, name=f"raw{a}_{i}")
                 grouped[a, i] = keep.tile([P, width, J], BF16, name=f"grouped{a}_{i}", align_bytes=256)
-                if (a, i) == (1, 2):
-                    load_scales(0)
-                    load_scales(1)
                 nc.sync.dma_start(out=raws[a, i][:], in_=x_view[a][:, :, t0 : t0 + width])
                 if (a, i) == (0, 0):
                     nc.sync.dma_start(offs_t[:], offs)
 
-        load_w8(0, 2)
-        load_scales(2)
-        load_scales(3)
+        load_w8(0, 1)
+        load_w4(0, 1)
+        for r in range(4):
+            load_scales(r)
         nc.sync.dma_start(out=bias[:], in_=b.rearrange("(n p) e -> p n e", p=P))
-        load_w4(0, 4)
-        load_w8(2, 4)
-        load_gate(0)
         nc.sync.dma_start(dst_t[:], dst)
+        load_gate(0, 2)
+        load_w8(1, 2)
+        load_w4(1, 4)
+        load_w8(2, 4)
+        load_gate(2, 8)
         load_w8(4, 6)
         load_w4(4, 8)
         load_w8(6, 8)
-        load_gate(1)
 
         def interleave(a, i):
             t0, width, v = CHUNKS[a][i]
             for copy, lo, hi in ((nc.vector.tensor_copy, 0, v), (nc.scalar.copy, v, width)):
+                if lo == hi:
+                    continue
                 copy(
                     out=grouped[a, i][:, lo:hi, :].rearrange("p (c i) j -> p c j i", i=4),
                     in_=raws[a, i][:, :, lo:hi].rearrange("p j (c i) -> p c j i", i=4),
@@ -116,19 +117,19 @@ def tile_moe_two_lin_relu2_kernel(tc, xT, w8_words, w8_scales, w4_words, w4_scal
         def gather(to, of, e0, e1):
             nc.vector.tensor_copy(to[:, e0 * C : e1 * C], of[:].indirect(offs_t[:, 8 * e0 : 8 * e1]))
 
-        interleave(0, 0)
-        interleave(0, 1)
-        quantise(0, 0)
-        quantise(0, 1)
-        gather(g_words[0], words[0], 0, 4)
-        gather(g_words[0], words[0], 4, 8)
+        for i in range(2):
+            interleave(0, i)
+            quantise(0, i)
+        gather(g_words[0], words[0], 0, 8)
         interleave(1, 0)
         interleave(1, 1)
         quantise(1, 0)
         interleave(1, 2)
         quantise(1, 1)
+        interleave(1, 3)
         quantise(1, 2)
-        for e0, e1 in ((0, 2), (2, 8)):
+        quantise(1, 3)
+        for e0, e1 in ((0, 4), (4, 8)):
             gather(g_scales, scales, e0, e1)
             gather(g_words[1], words[1], e0, e1)
 

@@ -21,8 +21,8 @@ MULT = mybir.AluOpType.mult
 NT = N // P
 HALF = T // 2
 CHUNKS = (
-    ((0, 512, 320), (512, 512, 320)),
-    ((0, 256, 0), (256, 256, 0), (512, 256, 96), (768, 256, 160)),
+    ((0, 512, 0, 4, 320), (512, 512, 0, 2, 336), (512, 512, 2, 2, 336)),
+    ((0, 256, 0, 4, 0), (256, 256, 0, 4, 0), (512, 256, 0, 4, 96), (768, 256, 0, 4, 160)),
 )
 PLANE = (4, 0)
 PIECES = (
@@ -72,12 +72,12 @@ def tile_moe_two_lin_relu2_kernel(tc, xT, w8_words, w8_scales, w4_words, w4_scal
             nc.sync.dma_start(out=gate_t[:, e0 * C : e1 * C], in_=gate[0:P, e0 * C : e1 * C])
 
         x_view = xT.rearrange("(a p j) t -> a p j t", a=2, j=J)
-        raws, grouped = {}, {}
+        raws = {}
+        grouped = [keep.tile([P, T * J], BF16, name=f"grouped{a}", align_bytes=256) for a in range(2)]
         for a in range(2):
-            for i, (t0, width, v) in enumerate(CHUNKS[a]):
-                raws[a, i] = keep.tile([P, J, width], F32, name=f"raw{a}_{i}")
-                grouped[a, i] = keep.tile([P, width, J], BF16, name=f"grouped{a}_{i}", align_bytes=256)
-                nc.sync.dma_start(out=raws[a, i][:], in_=x_view[a][:, :, t0 : t0 + width])
+            for i, (t0, width, j0, rows, v) in enumerate(CHUNKS[a]):
+                raws[a, i] = keep.tile([P, rows, width], F32, name=f"raw{a}_{i}")
+                nc.sync.dma_start(out=raws[a, i][:], in_=x_view[a][:, j0 : j0 + rows, t0 : t0 + width])
                 if (a, i) == (0, 0):
                     nc.sync.dma_start(offs_t[:], offs)
 
@@ -96,39 +96,45 @@ def tile_moe_two_lin_relu2_kernel(tc, xT, w8_words, w8_scales, w4_words, w4_scal
         load_w4(4, 8)
         load_w8(6, 8)
 
-        def interleave(a, i):
-            t0, width, v = CHUNKS[a][i]
-            for copy, lo, hi in ((nc.vector.tensor_copy, 0, v), (nc.scalar.copy, v, width)):
-                if lo == hi:
-                    continue
-                copy(
-                    out=grouped[a, i][:, lo:hi, :].rearrange("p (c i) j -> p c j i", i=4),
-                    in_=raws[a, i][:, :, lo:hi].rearrange("p j (c i) -> p c j i", i=4),
-                )
+        def round_tokens(copy, a, i, lo, hi):
+            t0, width, j0, rows, v = CHUNKS[a][i]
+            to = grouped[a][:, J * (t0 + lo) : J * (t0 + hi)].rearrange("p (c i j) -> p c j i", i=4, j=J)
+            copy(out=to[:, :, j0 : j0 + rows, :], in_=raws[a, i][:, :, lo:hi].rearrange("p j (c i) -> p c j i", i=4))
 
-        def quantise(a, i):
-            t0, width, v = CHUNKS[a][i]
+        def interleave(a, i, cut=0):
+            t0, width, j0, rows, v = CHUNKS[a][i]
+            for copy, lo, hi in (
+                (nc.vector.tensor_copy, 0, cut),
+                (nc.vector.tensor_copy, cut, v),
+                (nc.scalar.copy, v, width),
+            ):
+                if lo < hi:
+                    round_tokens(copy, a, i, lo, hi)
+
+        def quantise(a, t0, t1):
             nc.vector.quantize_mx(
-                out=words[a][:, t0 : t0 + width].bitcast(FP8X4),
-                scales=scales[PLANE[a] : P, t0 : t0 + width],
-                in_=grouped[a, i][:].rearrange("p t j -> p (t j)"),
+                out=words[a][:, t0:t1].bitcast(FP8X4),
+                scales=scales[PLANE[a] : P, t0:t1],
+                in_=grouped[a][:, J * t0 : J * t1],
             )
 
         def gather(to, of, e0, e1):
             nc.vector.tensor_copy(to[:, e0 * C : e1 * C], of[:].indirect(offs_t[:, 8 * e0 : 8 * e1]))
 
-        for i in range(2):
-            interleave(0, i)
-            quantise(0, i)
+        interleave(0, 0)
+        quantise(0, 0, 512)
+        interleave(0, 1)
+        interleave(0, 2, 256)
+        quantise(0, 512, 768)
+        quantise(0, 768, 1024)
         gather(g_words[0], words[0], 0, 8)
         interleave(1, 0)
         interleave(1, 1)
-        quantise(1, 0)
+        quantise(1, 0, 512)
         interleave(1, 2)
-        quantise(1, 1)
         interleave(1, 3)
-        quantise(1, 2)
-        quantise(1, 3)
+        quantise(1, 512, 768)
+        quantise(1, 768, 1024)
         for e0, e1 in ((0, 4), (4, 8)):
             gather(g_scales, scales, e0, e1)
             gather(g_words[1], words[1], e0, e1)

@@ -21,8 +21,8 @@ MULT = mybir.AluOpType.mult
 NT = N // P
 HALF = T // 2
 CHUNKS = (
-    ((0, 512, 0, 4, 320), (512, 512, 0, 2, 336), (512, 512, 2, 2, 336)),
-    ((0, 256, 0, 4, 0), (256, 256, 0, 4, 0), (512, 256, 0, 4, 96), (768, 256, 0, 4, 160)),
+    ((0, 1024, 0, 2, 512), (0, 1024, 2, 2, 512)),
+    ((0, 256, 0, 4, 0), (256, 256, 0, 4, 0), (512, 256, 0, 4, 0), (768, 256, 0, 4, 176)),
 )
 PLANE = (4, 0)
 PIECES = (
@@ -78,7 +78,7 @@ def tile_moe_two_lin_relu2_kernel(tc, xT, w8_words, w8_scales, w4_words, w4_scal
             for i, (t0, width, j0, rows, v) in enumerate(CHUNKS[a]):
                 raws[a, i] = keep.tile([P, rows, width], F32, name=f"raw{a}_{i}")
                 nc.sync.dma_start(out=raws[a, i][:], in_=x_view[a][:, j0 : j0 + rows, t0 : t0 + width])
-                if (a, i) == (0, 0):
+                if (a, i) == (0, 1):
                     nc.sync.dma_start(offs_t[:], offs)
 
         load_w8(0, 1)
@@ -122,11 +122,10 @@ def tile_moe_two_lin_relu2_kernel(tc, xT, w8_words, w8_scales, w4_words, w4_scal
             nc.vector.tensor_copy(to[:, e0 * C : e1 * C], of[:].indirect(offs_t[:, 8 * e0 : 8 * e1]))
 
         interleave(0, 0)
-        quantise(0, 0, 512)
-        interleave(0, 1)
-        interleave(0, 2, 256)
-        quantise(0, 512, 768)
-        quantise(0, 768, 1024)
+        for q in range(4):
+            round_tokens(nc.vector.tensor_copy if q < 2 else nc.scalar.copy, 0, 1, 256 * q, 256 * (q + 1))
+        for q in range(4):
+            quantise(0, 256 * q, 256 * (q + 1))
         gather(g_words[0], words[0], 0, 8)
         interleave(1, 0)
         interleave(1, 1)

@@ -22,11 +22,11 @@ NT = N // P
 HALF = T // 2
 CHUNKS = (
     ((0, 1024, 0, 2, 512), (0, 1024, 2, 2, 512)),
-    ((0, 256, 0, 4, 0), (256, 256, 0, 4, 0), (512, 256, 0, 4, 0), (768, 256, 0, 4, 176)),
+    ((0, 256, 0, 4, 0), (256, 256, 0, 4, 0), (512, 256, 0, 4, 0), (768, 256, 0, 4, 208)),
 )
 PLANE = (4, 0)
 PIECES = (
-    (0, 0, 1), (1, 0, 1), (2, 0, 2), (3, 0, 2), (0, 1, 4), (1, 1, 4), (2, 2, 8), (3, 2, 8), (0, 4, 8), (1, 4, 8),
+    (0, 0, 1), (1, 0, 2), (2, 0, 2), (0, 1, 4), (3, 0, 4), (0, 4, 8), (1, 2, 8), (2, 2, 8), (3, 4, 8),
 )
 
 
@@ -44,7 +44,7 @@ def tile_moe_two_lin_relu2_kernel(tc, xT, w8_words, w8_scales, w4_words, w4_scal
         w8_t = keep.tile([P, E, 4 * N], U8, name="w8_t", align_bytes=256)
         w4_t = keep.tile([P, E, 2 * N], U8, name="w4_t", align_bytes=256)
         w_sc = keep.tile([P, E * N], U8, name="w_sc", align_bytes=256)
-        window = [keep.tile([P, T if n < 2 else 2 * T], F32, name=f"window{n}") for n in range(NT)]
+        window = [keep.tile([P, 2 * T if n in (1, 2) else T], F32, name=f"window{n}") for n in range(NT)]
         banks = [[psum.tile([P, HALF], F32, name=f"bank{n}_{h}") for h in range(2)] for n in range(NT)]
 
         nc.gpsimd.memset(scales[:], 0)
@@ -82,19 +82,20 @@ def tile_moe_two_lin_relu2_kernel(tc, xT, w8_words, w8_scales, w4_words, w4_scal
                     nc.sync.dma_start(offs_t[:], offs)
 
         load_w8(0, 1)
-        load_w4(0, 1)
+        load_w4(0, 2)
         for r in range(4):
             load_scales(r)
         nc.sync.dma_start(out=bias[:], in_=b.rearrange("(n p) e -> p n e", p=P))
+        load_w8(1, 2)
         nc.sync.dma_start(dst_t[:], dst)
         load_gate(0, 2)
-        load_w8(1, 2)
-        load_w4(1, 4)
+        load_w4(2, 4)
         load_w8(2, 4)
-        load_gate(2, 8)
+        load_gate(2, 4)
         load_w8(4, 6)
         load_w4(4, 8)
         load_w8(6, 8)
+        load_gate(4, 8)
 
         def round_tokens(copy, a, i, lo, hi):
             t0, width, j0, rows, v = CHUNKS[a][i]
@@ -134,7 +135,7 @@ def tile_moe_two_lin_relu2_kernel(tc, xT, w8_words, w8_scales, w4_words, w4_scal
         interleave(1, 3)
         quantise(1, 512, 768)
         quantise(1, 768, 1024)
-        for e0, e1 in ((0, 4), (4, 8)):
+        for e0, e1 in ((0, 2), (2, 8)):
             gather(g_scales, scales, e0, e1)
             gather(g_words[1], words[1], e0, e1)
 

@@ -22,7 +22,7 @@ NT = N // P
 HALF = T // 2
 CHUNKS = (
     ((0, 1024, 0, 2, 512), (0, 1024, 2, 2, 512)),
-    ((0, 256, 0, 4, 0), (256, 256, 0, 4, 0), (512, 256, 0, 4, 0), (768, 256, 0, 4, 208)),
+    ((0, 512, 0, 4, 0), (512, 256, 0, 4, 0), (768, 256, 0, 4, 208)),
 )
 PLANE = (4, 0)
 PIECES = (
@@ -128,11 +128,16 @@ def tile_moe_two_lin_relu2_kernel(tc, xT, w8_words, w8_scales, w4_words, w4_scal
         for q in range(4):
             quantise(0, 256 * q, 256 * (q + 1))
         gather(g_words[0], words[0], 0, 8)
-        interleave(1, 0)
+        reused = grouped[0][:, J * 768 : J * 1024]
+        nc.gpsimd.tensor_copy(
+            out=reused.rearrange("p (t j) -> p t j", j=J),
+            in_=raws[1, 0][:, :, 0:256].rearrange("p j t -> p t j"),
+        )
+        round_tokens(nc.scalar.copy, 1, 0, 256, 512)
+        quantise(1, 256, 512)
+        nc.vector.quantize_mx(out=words[1][:, 0:256].bitcast(FP8X4), scales=scales[:, 0:256], in_=reused)
         interleave(1, 1)
-        quantise(1, 0, 512)
         interleave(1, 2)
-        interleave(1, 3)
         quantise(1, 512, 768)
         quantise(1, 768, 1024)
         for e0, e1 in ((0, 2), (2, 8)):

@@ -21,13 +21,11 @@ MULT = mybir.AluOpType.mult
 NT = N // P
 HALF = T // 2
 CHUNKS = (
-    ((0, 1024, 0, 2, 512), (0, 1024, 2, 2, 512)),
-    ((0, 512, 0, 4, 0), (512, 256, 0, 4, 0), (768, 256, 0, 4, 208)),
+    ((0, 1024, 0, 2, 0), (0, 512, 2, 2, 336), (512, 512, 2, 2, 336)),
+    ((0, 512, 0, 4, 0), (512, 256, 0, 4, 0), (768, 256, 0, 4, 160)),
 )
 PLANE = (4, 0)
-PIECES = (
-    (0, 0, 1), (1, 0, 2), (2, 0, 2), (0, 1, 4), (3, 0, 4), (0, 4, 8), (1, 2, 8), (2, 2, 8), (3, 4, 8),
-)
+PIECES = ((0, 0, 2), (1, 0, 2), (2, 0, 4), (3, 0, 8), (0, 2, 8), (1, 2, 8), (2, 4, 8))
 
 
 def tile_moe_two_lin_relu2_kernel(tc, xT, w8_words, w8_scales, w4_words, w4_scales, b, gate, offs, dst, out):
@@ -44,7 +42,7 @@ def tile_moe_two_lin_relu2_kernel(tc, xT, w8_words, w8_scales, w4_words, w4_scal
         w8_t = keep.tile([P, E, 4 * N], U8, name="w8_t", align_bytes=256)
         w4_t = keep.tile([P, E, 2 * N], U8, name="w4_t", align_bytes=256)
         w_sc = keep.tile([P, E * N], U8, name="w_sc", align_bytes=256)
-        window = [keep.tile([P, 2 * T if n in (1, 2) else T], F32, name=f"window{n}") for n in range(NT)]
+        window = [keep.tile([P, T if n == 2 else 2 * T], F32, name=f"window{n}") for n in range(NT)]
         banks = [[psum.tile([P, HALF], F32, name=f"bank{n}_{h}") for h in range(2)] for n in range(NT)]
 
         nc.gpsimd.memset(scales[:], 0)
@@ -61,12 +59,12 @@ def tile_moe_two_lin_relu2_kernel(tc, xT, w8_words, w8_scales, w4_words, w4_scal
                 out=w4_t[:, e0:e1, :].bitcast(I32), in_=w4_words[e0:e1].rearrange("e a p n -> (a p) e n").bitcast(I32)
             )
 
-        def load_scales(r):
-            for plane, sc in ((0, w4_scales), (4, w8_scales)):
-                nc.sync.dma_start(
-                    out=w_sc[plane + r : P : 32, :].bitcast(I32).rearrange("q (e n) -> q e n", e=E),
-                    in_=sc.bitcast(I32).rearrange("e a (q r) n -> r a q e n", r=4)[r][0],
-                )
+        def load_scales(i):
+            plane, sc = ((0, w4_scales), (4, w8_scales))[i % 2]
+            nc.sync.dma_start(
+                out=w_sc[plane + i // 2 : P : 32, :].bitcast(I32).rearrange("q (e n) -> q e n", e=E),
+                in_=sc.bitcast(I32).rearrange("e a (q r) n -> r a q e n", r=4)[i // 2][0],
+            )
 
         def load_gate(e0, e1):
             nc.sync.dma_start(out=gate_t[:, e0 * C : e1 * C], in_=gate[0:P, e0 * C : e1 * C])
@@ -78,19 +76,20 @@ def tile_moe_two_lin_relu2_kernel(tc, xT, w8_words, w8_scales, w4_words, w4_scal
             for i, (t0, width, j0, rows, v) in enumerate(CHUNKS[a]):
                 raws[a, i] = keep.tile([P, rows, width], F32, name=f"raw{a}_{i}")
                 nc.sync.dma_start(out=raws[a, i][:], in_=x_view[a][:, j0 : j0 + rows, t0 : t0 + width])
-                if (a, i) == (0, 1):
+                if (a, i) == (0, 2):
                     nc.sync.dma_start(offs_t[:], offs)
 
-        load_w8(0, 1)
+        for i in range(2):
+            load_scales(i)
+        load_w8(0, 2)
         load_w4(0, 2)
-        for r in range(4):
-            load_scales(r)
+        for i in range(2, 8):
+            load_scales(i)
         nc.sync.dma_start(out=bias[:], in_=b.rearrange("(n p) e -> p n e", p=P))
-        load_w8(1, 2)
+        load_w8(2, 4)
         nc.sync.dma_start(dst_t[:], dst)
         load_gate(0, 2)
         load_w4(2, 4)
-        load_w8(2, 4)
         load_gate(2, 4)
         load_w8(4, 6)
         load_w4(4, 8)
@@ -122,20 +121,26 @@ def tile_moe_two_lin_relu2_kernel(tc, xT, w8_words, w8_scales, w4_words, w4_scal
         def gather(to, of, e0, e1):
             nc.vector.tensor_copy(to[:, e0 * C : e1 * C], of[:].indirect(offs_t[:, 8 * e0 : 8 * e1]))
 
-        interleave(0, 0)
-        for q in range(4):
-            round_tokens(nc.vector.tensor_copy if q < 2 else nc.scalar.copy, 0, 1, 256 * q, 256 * (q + 1))
-        for q in range(4):
-            quantise(0, 256 * q, 256 * (q + 1))
+        for t0 in (0, 512):
+            round_tokens(nc.vector.tensor_copy, 0, 0, t0, t0 + 336)
+            round_tokens(nc.scalar.copy, 0, 0, t0 + 336, t0 + 512)
+        for h in range(2):
+            interleave(0, 1 + h, cut=256)
+            if h == 0:
+                quantise(0, 0, 512)
+        quantise(0, 512, 768)
+        quantise(0, 768, 1024)
         gather(g_words[0], words[0], 0, 8)
-        reused = grouped[0][:, J * 768 : J * 1024]
+        reused = grouped[0][:, J * 512 : J * 1024]
         nc.gpsimd.tensor_copy(
-            out=reused.rearrange("p (t j) -> p t j", j=J),
-            in_=raws[1, 0][:, :, 0:256].rearrange("p j t -> p t j"),
+            out=reused[:, J * 256 : J * 512].rearrange("p (t j) -> p t j", j=J),
+            in_=raws[1, 0][:, :, 256:512].rearrange("p j t -> p t j"),
         )
-        round_tokens(nc.scalar.copy, 1, 0, 256, 512)
-        quantise(1, 256, 512)
-        nc.vector.quantize_mx(out=words[1][:, 0:256].bitcast(FP8X4), scales=scales[:, 0:256], in_=reused)
+        nc.scalar.copy(
+            out=reused[:, 0 : J * 256].rearrange("p (c i j) -> p c j i", i=4, j=J),
+            in_=raws[1, 0][:, :, 0:256].rearrange("p j (c i) -> p c j i", i=4),
+        )
+        nc.vector.quantize_mx(out=words[1][:, 0:512].bitcast(FP8X4), scales=scales[:, 0:512], in_=reused)
         interleave(1, 1)
         interleave(1, 2)
         quantise(1, 512, 768)

@@ -15,8 +15,11 @@ U8 = mybir.dt.uint8
 FP8X4 = mybir.dt.float8_e4m3fn_x4
 FP4X4 = mybir.dt.float4_e2m1fn_x4
 RELU = mybir.ActivationFunctionType.Relu
+COPY = mybir.ActivationFunctionType.Copy
 SQUARE = mybir.ActivationFunctionType.Square
 MULT = mybir.AluOpType.mult
+ADD = mybir.AluOpType.add
+MAX = mybir.AluOpType.max
 
 NT = N // P
 HALF = T // 2
@@ -25,7 +28,10 @@ CHUNKS = (
     ((0, 512, 0, 4, 0), (512, 256, 0, 4, 0), (768, 256, 0, 4, 160)),
 )
 PLANE = (4, 0)
-PIECES = ((0, 0, 2), (1, 0, 2), (2, 0, 4), (3, 0, 8), (0, 2, 8), (1, 2, 8), (2, 4, 8))
+PIECES = ((0, 0), (1, 0), (0, 1), (1, 1), (0, 2), (0, 3), (1, 2), (1, 3))
+EARLY = 4
+LAST = len(PIECES) - 1
+W = 2 * C
 
 
 def tile_moe_two_lin_relu2_kernel(tc, xT, w8_words, w8_scales, w4_words, w4_scales, b, gate, offs, dst, out):
@@ -33,7 +39,6 @@ def tile_moe_two_lin_relu2_kernel(tc, xT, w8_words, w8_scales, w4_words, w4_scal
     with tc.tile_pool(name="keep", bufs=1) as keep, tc.psum_pool(name="psum", bufs=1) as psum:
         offs_t = keep.tile([P, 64], U16, name="offs_t")
         dst_t = keep.tile([P, 64], U16, name="dst_t")
-        bias = keep.tile([P, NT, E], F32, name="bias")
         gate_t = keep.tile([P, T], F32, name="gate_t")
         words = [keep.tile([P, 2 * T if a == 0 else T], U32, name=f"words{a}", align_bytes=256) for a in range(2)]
         scales = keep.tile([P, T], U8, name="scales", align_bytes=256)
@@ -42,8 +47,8 @@ def tile_moe_two_lin_relu2_kernel(tc, xT, w8_words, w8_scales, w4_words, w4_scal
         w8_t = keep.tile([P, E, 4 * N], U8, name="w8_t", align_bytes=256)
         w4_t = keep.tile([P, E, 2 * N], U8, name="w4_t", align_bytes=256)
         w_sc = keep.tile([P, E * N], U8, name="w_sc", align_bytes=256)
-        window = [keep.tile([P, T if n == 2 else 2 * T], F32, name=f"window{n}") for n in range(NT)]
-        banks = [[psum.tile([P, HALF], F32, name=f"bank{n}_{h}") for h in range(2)] for n in range(NT)]
+        window = [keep.tile([P, T + NT * E], F32, name=f"window{n}") for n in range(NT)]
+        bias = keep.tile([P, NT * E], F32, name="bias")
 
         nc.gpsimd.memset(scales[:], 0)
         nc.vector.memset(w_sc[:].bitcast(I32), 0)
@@ -79,16 +84,16 @@ def tile_moe_two_lin_relu2_kernel(tc, xT, w8_words, w8_scales, w4_words, w4_scal
                 if (a, i) == (0, 2):
                     nc.sync.dma_start(offs_t[:], offs)
 
-        for i in range(2):
+        for i in range(5):
             load_scales(i)
         load_w8(0, 2)
         load_w4(0, 2)
-        for i in range(2, 8):
+        nc.sync.dma_start(out=bias[:].rearrange("p (n e) -> p n e", e=E), in_=b.rearrange("(n p) e -> p n e", p=P))
+        for i in range(5, 8):
             load_scales(i)
-        nc.sync.dma_start(out=bias[:], in_=b.rearrange("(n p) e -> p n e", p=P))
-        load_w8(2, 4)
-        nc.sync.dma_start(dst_t[:], dst)
         load_gate(0, 2)
+        nc.sync.dma_start(dst_t[:], dst)
+        load_w8(2, 4)
         load_w4(2, 4)
         load_gate(2, 4)
         load_w8(4, 6)
@@ -145,21 +150,37 @@ def tile_moe_two_lin_relu2_kernel(tc, xT, w8_words, w8_scales, w4_words, w4_scal
         interleave(1, 2)
         quantise(1, 512, 768)
         quantise(1, 768, 1024)
-        for e0, e1 in ((0, 2), (2, 8)):
+        for e0, e1 in ((0, 1), (1, 2), (2, 4), (4, 8)):
             gather(g_scales, scales, e0, e1)
             gather(g_words[1], words[1], e0, e1)
 
-        for n, e0, e1 in PIECES:
-            width = (e1 - e0) * C
-            relu = keep.tile([P, width], F32, name=f"relu{n}_{e0}")
-            squared = keep.tile([P, width], F32, name=f"squared{n}_{e0}")
-            for e in range(e0, e1):
-                bank = banks[n][e // 4]
-                place = slice(e % 4 * C, (e % 4 + 1) * C)
+        banks = [psum.tile([P, 2, W], F32, name=f"bank{i}") for i in range(len(PIECES))]
+        relu = [keep.tile([P, 2, W], F32, name=f"relu{i}") for i in range(len(PIECES))]
+        other = [keep.tile([P, 2, W], F32, name=f"other{i}") for i in range(len(PIECES))]
+        gated = [keep.tile([P, 2, W], F32, name=f"gated{i}") for i in range(len(PIECES))]
+
+        for n in (1, 3, 0, 2):
+            nc.gpsimd.tensor_copy(window[n][:, T : T + NT * E], bias[:])
+
+        def bias_of(holder, n, e):
+            if holder is None:
+                return bias[:, n * E + e : n * E + e + 1]
+            return window[holder][:, T + n * E + e : T + n * E + e + 1]
+
+        def blocks(i):
+            m, g = PIECES[i]
+            return [(h, 2 * m + h, 2 * g + d, slice(d * C, (d + 1) * C)) for d in range(2) for h in range(2)]
+
+        def sums(i, h, place):
+            bank = banks[LAST] if i == 0 and place.start else banks[i]
+            return bank[:, h, place]
+
+        def multiply(i):
+            for h, n, e, place in blocks(i):
                 slots = slice(e * C, (e + 1) * C)
                 w_cols = slice(e * N + n * P, e * N + (n + 1) * P)
                 nc.tensor.matmul_mx(
-                    out=bank[:, place],
+                    out=sums(i, h, place),
                     lhsT=w8_t[:, e, 4 * n * P : 4 * (n + 1) * P].bitcast(FP8X4),
                     lhsT_scale=w_sc[4:P, w_cols],
                     rhs=g_words[0][:, slots].bitcast(FP8X4),
@@ -168,7 +189,7 @@ def tile_moe_two_lin_relu2_kernel(tc, xT, w8_words, w8_scales, w4_words, w4_scal
                     stop=False,
                 )
                 nc.tensor.matmul_mx(
-                    out=bank[:, place],
+                    out=sums(i, h, place),
                     lhsT=w4_t[:, e, 2 * n * P : 2 * (n + 1) * P].bitcast(FP4X4),
                     lhsT_scale=w_sc[:, w_cols],
                     rhs=g_words[1][:, slots].bitcast(FP8X4),
@@ -176,15 +197,59 @@ def tile_moe_two_lin_relu2_kernel(tc, xT, w8_words, w8_scales, w4_words, w4_scal
                     start=False,
                     stop=True,
                 )
-            for e in range(e0, e1):
-                bank = banks[n][e // 4]
-                place = slice(e % 4 * C, (e % 4 + 1) * C)
-                nc.scalar.activation(
-                    relu[:, (e - e0) * C : (e - e0 + 1) * C], bank[:, place], RELU, bias=bias[:, n, e : e + 1]
+
+        def gate_product(i):
+            g = PIECES[i][1]
+            if i == LAST:
+                nc.gpsimd.tensor_tensor(gated[i][:, 1, :], other[i][:, 1, :], gate_t[:, g * W : (g + 1) * W], MULT)
+                return
+            weights = gate_t[:, g * W : (g + 1) * W].unsqueeze(1).to_broadcast([P, 2, W])
+            nc.gpsimd.tensor_tensor(gated[i][:], other[i][:], weights, MULT)
+
+        def early_piece(i):
+            for h, n, e, place in blocks(i):
+                nc.scalar.activation(relu[i][:, h, place], sums(i, h, place), RELU, bias=bias_of(2 * h + 1 if i >= 2 else None, n, e))
+            nc.scalar.activation(other[i][:], relu[i][:], SQUARE)
+            gate_product(i)
+
+        def vector_relu(i):
+            for h, n, e, place in blocks(i):
+                nc.vector.tensor_scalar(relu[i][:, h, place], sums(i, h, place), bias_of(2 * h, n, e), 0.0, ADD, MAX)
+
+        def products(i):
+            nc.gpsimd.tensor_tensor(other[i][:], relu[i][:], relu[i][:], MULT)
+            gate_product(i)
+
+        def late_piece(i):
+            vector_relu(i)
+            products(i)
+
+        def scatter(i):
+            m, g = PIECES[i]
+            places = dst_t[:, 16 * g : 16 * (g + 1)]
+            if i == LAST:
+                nc.vector.tensor_tensor(
+                    window[2 * m][:].indirect(places), other[i][:, 0, :], gate_t[:, g * W : (g + 1) * W], MULT
                 )
-            nc.scalar.activation(squared[:], relu[:], SQUARE)
-            nc.vector.tensor_tensor(
-                window[n][:].indirect(dst_t[:, 8 * e0 : 8 * e1]), squared[:], gate_t[:, e0 * C : e1 * C], MULT
-            )
-            if e1 == E:
-                nc.sync.dma_start(out=out[n * P : (n + 1) * P, :], in_=window[n][:, 0:T])
+            else:
+                nc.vector.tensor_copy(window[2 * m][:].indirect(places), gated[i][:, 0, :])
+            nc.scalar.activation(window[2 * m + 1][:].indirect(places), gated[i][:, 1, :], COPY)
+            if g == 3:
+                for n in (2 * m + 1, 2 * m):
+                    nc.sync.dma_start(out=out[n * P : (n + 1) * P, :], in_=window[n][:, 0:T])
+
+        for i in range(EARLY):
+            multiply(i)
+            early_piece(i)
+        for i in range(EARLY, len(PIECES)):
+            multiply(i)
+        scatter(0)
+        late_piece(4)
+        vector_relu(6)
+        scatter(1)
+        late_piece(5)
+        vector_relu(7)
+        for i in (6, 7):
+            products(i)
+        for i in range(2, len(PIECES)):
+            scatter(i)

@@ -220,9 +220,13 @@ def tile_moe_two_lin_relu2_kernel(tc, xT, w8_words, w8_scales, w4_words, w4_scal
             nc.gpsimd.tensor_tensor(other[i][:], relu[i][:], relu[i][:], MULT)
             gate_product(i)
 
-        def late_piece(i):
+        def gated_piece(i):
             vector_relu(i)
-            products(i)
+            for h, n, e, place in blocks(i):
+                nc.vector.scalar_tensor_tensor(
+                    other[i][:, h, place], sums(i, h, place), bias_of(2 * h, n, e), gate_t[:, e * C : (e + 1) * C], ADD, MULT
+                )
+            nc.gpsimd.tensor_tensor(gated[i][:], other[i][:], relu[i][:], MULT)
 
         def scatter(i):
             m, g = PIECES[i]
@@ -244,10 +248,10 @@ def tile_moe_two_lin_relu2_kernel(tc, xT, w8_words, w8_scales, w4_words, w4_scal
         for i in range(EARLY, len(PIECES)):
             multiply(i)
         scatter(0)
-        late_piece(4)
+        gated_piece(4)
         vector_relu(6)
         scatter(1)
-        late_piece(5)
+        gated_piece(5)
         vector_relu(7)
         for i in (6, 7):
             products(i)

@@ -29,6 +29,7 @@ CHUNKS = (
 )
 PLANE = (4, 0)
 PIECES = ((0, 0), (1, 0), (0, 1), (1, 1), (0, 2), (0, 3), (1, 2), (1, 3))
+RUNS = ((0, 0, 2), (0, 2, 8), (1, 0, 2), (1, 2, 4), (1, 4, 6), (1, 6, 8))
 EARLY = 4
 LAST = len(PIECES) - 1
 W = 2 * C
@@ -83,18 +84,18 @@ def tile_moe_two_lin_relu2_kernel(tc, xT, w8_words, w8_scales, w4_words, w4_scal
                 nc.sync.dma_start(out=raws[a, i][:], in_=x_view[a][:, j0 : j0 + rows, t0 : t0 + width])
                 if (a, i) == (0, 2):
                     nc.sync.dma_start(offs_t[:], offs)
+                    nc.sync.dma_start(out=bias[:].rearrange("p (n e) -> p n e", e=E), in_=b.rearrange("(n p) e -> p n e", p=P))
 
         for i in range(5):
             load_scales(i)
         load_w8(0, 2)
         load_w4(0, 2)
-        nc.sync.dma_start(out=bias[:].rearrange("p (n e) -> p n e", e=E), in_=b.rearrange("(n p) e -> p n e", p=P))
         for i in range(5, 8):
             load_scales(i)
-        load_gate(0, 2)
-        nc.sync.dma_start(dst_t[:], dst)
         load_w8(2, 4)
+        load_gate(0, 2)
         load_w4(2, 4)
+        nc.sync.dma_start(dst_t[:], dst)
         load_gate(2, 4)
         load_w8(4, 6)
         load_w4(4, 8)
@@ -150,14 +151,15 @@ def tile_moe_two_lin_relu2_kernel(tc, xT, w8_words, w8_scales, w4_words, w4_scal
         interleave(1, 2)
         quantise(1, 512, 768)
         quantise(1, 768, 1024)
-        for e0, e1 in ((0, 1), (1, 2), (2, 4), (4, 8)):
+        for e0, e1 in ((0, 2), (2, 4), (4, 8)):
             gather(g_scales, scales, e0, e1)
             gather(g_words[1], words[1], e0, e1)
 
         banks = [psum.tile([P, 2, W], F32, name=f"bank{i}") for i in range(len(PIECES))]
         relu = [keep.tile([P, 2, W], F32, name=f"relu{i}") for i in range(len(PIECES))]
-        other = [keep.tile([P, 2, W], F32, name=f"other{i}") for i in range(len(PIECES))]
-        gated = [keep.tile([P, 2, W], F32, name=f"gated{i}") for i in range(len(PIECES))]
+        other = [keep.tile([P, 2, W], F32, name=f"other{i}") for i in range(6)]
+        other = other + [other[5], other[5]]
+        gated = {run: keep.tile([P, 2, (run[2] - run[1]) * C], F32, name=f"gated{run[0]}_{run[1]}") for run in RUNS}
 
         for n in (1, 3, 0, 2):
             nc.gpsimd.tensor_copy(window[n][:, T : T + NT * E], bias[:])
@@ -198,62 +200,91 @@ def tile_moe_two_lin_relu2_kernel(tc, xT, w8_words, w8_scales, w4_words, w4_scal
                     stop=True,
                 )
 
-        def gate_product(i):
-            g = PIECES[i][1]
-            if i == LAST:
-                nc.gpsimd.tensor_tensor(gated[i][:, 1, :], other[i][:, 1, :], gate_t[:, g * W : (g + 1) * W], MULT)
-                return
-            weights = gate_t[:, g * W : (g + 1) * W].unsqueeze(1).to_broadcast([P, 2, W])
-            nc.gpsimd.tensor_tensor(gated[i][:], other[i][:], weights, MULT)
+        def results(m, e0, e1):
+            run = [r for r in RUNS if r[0] == m and r[1] <= e0 < r[2]][0]
+            return gated[run][:, :, (e0 - run[1]) * C : (e1 - run[1]) * C]
 
-        def early_piece(i):
+        def result(i):
+            m, g = PIECES[i]
+            return results(m, 2 * g, 2 * g + 2)
+
+        def gate_of(i):
+            g = PIECES[i][1]
+            return gate_t[:, g * W : (g + 1) * W]
+
+        def gate_product(i):
+            if i == LAST:
+                nc.gpsimd.tensor_tensor(result(i)[:, 1, :], other[i][:, 1, :], gate_of(i), MULT)
+            else:
+                nc.gpsimd.tensor_tensor(result(i), other[i][:], gate_of(i).unsqueeze(1).to_broadcast([P, 2, W]), MULT)
+
+        def scalar_relu(i):
             for h, n, e, place in blocks(i):
-                nc.scalar.activation(relu[i][:, h, place], sums(i, h, place), RELU, bias=bias_of(2 * h + 1 if i >= 2 else None, n, e))
-            nc.scalar.activation(other[i][:], relu[i][:], SQUARE)
-            gate_product(i)
+                holder = 2 * h + 1 if i >= 2 else None
+                nc.scalar.activation(relu[i][:, h, place], sums(i, h, place), RELU, bias=bias_of(holder, n, e))
 
         def vector_relu(i):
             for h, n, e, place in blocks(i):
                 nc.vector.tensor_scalar(relu[i][:, h, place], sums(i, h, place), bias_of(2 * h, n, e), 0.0, ADD, MAX)
 
-        def products(i):
-            nc.gpsimd.tensor_tensor(other[i][:], relu[i][:], relu[i][:], MULT)
+        def scalar_square(i):
+            nc.scalar.activation(other[i][:], relu[i][:], SQUARE)
             gate_product(i)
 
-        def gated_piece(i):
-            vector_relu(i)
+        def vector_gate(i):
             for h, n, e, place in blocks(i):
                 nc.vector.scalar_tensor_tensor(
                     other[i][:, h, place], sums(i, h, place), bias_of(2 * h, n, e), gate_t[:, e * C : (e + 1) * C], ADD, MULT
                 )
-            nc.gpsimd.tensor_tensor(gated[i][:], other[i][:], relu[i][:], MULT)
+            nc.gpsimd.tensor_tensor(result(i), other[i][:], relu[i][:], MULT)
 
-        def scatter(i):
-            m, g = PIECES[i]
-            places = dst_t[:, 16 * g : 16 * (g + 1)]
-            if i == LAST:
-                nc.vector.tensor_tensor(
-                    window[2 * m][:].indirect(places), other[i][:, 0, :], gate_t[:, g * W : (g + 1) * W], MULT
-                )
-            else:
-                nc.vector.tensor_copy(window[2 * m][:].indirect(places), gated[i][:, 0, :])
-            nc.scalar.activation(window[2 * m + 1][:].indirect(places), gated[i][:, 1, :], COPY)
-            if g == 3:
-                for n in (2 * m + 1, 2 * m):
-                    nc.sync.dma_start(out=out[n * P : (n + 1) * P, :], in_=window[n][:, 0:T])
+        def gpsimd_square(i):
+            nc.gpsimd.tensor_tensor(other[i][:], relu[i][:], relu[i][:], MULT)
+            gate_product(i)
+
+        def vector_scatter(m, e0, e1):
+            nc.vector.tensor_copy(window[2 * m][:].indirect(dst_t[:, 8 * e0 : 8 * e1]), results(m, e0, e1)[:, 0, :])
+
+        def scalar_scatter(m, e0, e1):
+            nc.scalar.activation(
+                window[2 * m + 1][:].indirect(dst_t[:, 8 * e0 : 8 * e1]), results(m, e0, e1)[:, 1, :], COPY
+            )
+
+        def store(n):
+            nc.sync.dma_start(out=out[n * P : (n + 1) * P, :], in_=window[n][:, 0:T])
 
         for i in range(EARLY):
             multiply(i)
-            early_piece(i)
+            scalar_relu(i)
+            if i == 1:
+                vector_gate(i)
+            else:
+                scalar_square(i)
         for i in range(EARLY, len(PIECES)):
             multiply(i)
-        scatter(0)
-        gated_piece(4)
-        vector_relu(6)
-        scatter(1)
-        gated_piece(5)
+        vector_scatter(0, 0, 2)
+        scalar_scatter(0, 0, 2)
+        vector_relu(4)
+        vector_gate(4)
+        scalar_relu(6)
+        vector_scatter(1, 0, 2)
+        scalar_scatter(1, 0, 2)
+        vector_relu(5)
+        vector_gate(5)
         vector_relu(7)
-        for i in (6, 7):
-            products(i)
-        for i in range(2, len(PIECES)):
-            scatter(i)
+        gpsimd_square(6)
+        gpsimd_square(7)
+        vector_scatter(0, 2, 4)
+        vector_scatter(1, 2, 4)
+        scalar_scatter(1, 2, 4)
+        scalar_scatter(0, 2, 5)
+        scalar_scatter(0, 5, 8)
+        store(1)
+        vector_scatter(0, 4, 8)
+        store(0)
+        vector_scatter(1, 4, 6)
+        scalar_scatter(1, 4, 6)
+        scalar_scatter(1, 6, 8)
+        store(3)
+        nc.vector.tensor_tensor(window[2][:].indirect(dst_t[:, 48:64]), other[LAST][:, 0, :], gate_of(LAST), MULT)
+        store(2)

@@ -28,11 +28,9 @@ CHUNKS = (
     ((0, 512, 0, 4, 0), (512, 256, 0, 4, 0), (768, 256, 0, 4, 160)),
 )
 PLANE = (4, 0)
-PIECES = ((0, 0), (1, 0), (0, 1), (1, 1), (0, 2), (0, 3), (1, 2), (1, 3))
-RUNS = ((0, 0, 2), (0, 2, 8), (1, 0, 2), (1, 2, 4), (1, 4, 6), (1, 6, 8))
-EARLY = 4
+PIECES = tuple((m, e0, e1) for e0, e1 in ((0, 2), (2, 5), (5, 8)) for m in range(2))
 LAST = len(PIECES) - 1
-W = 2 * C
+BANK = 512
 
 
 def tile_moe_two_lin_relu2_kernel(tc, xT, w8_words, w8_scales, w4_words, w4_scales, b, gate, offs, dst, out):
@@ -92,15 +90,14 @@ def tile_moe_two_lin_relu2_kernel(tc, xT, w8_words, w8_scales, w4_words, w4_scal
         load_w4(0, 2)
         for i in range(5, 8):
             load_scales(i)
-        load_w8(2, 4)
+        load_w8(2, 5)
         load_gate(0, 2)
-        load_w4(2, 4)
+        load_w4(2, 5)
         nc.sync.dma_start(dst_t[:], dst)
-        load_gate(2, 4)
-        load_w8(4, 6)
-        load_w4(4, 8)
-        load_w8(6, 8)
-        load_gate(4, 8)
+        load_gate(2, 5)
+        load_w8(5, 8)
+        load_w4(5, 8)
+        load_gate(5, 8)
 
         def round_tokens(copy, a, i, lo, hi):
             t0, width, j0, rows, v = CHUNKS[a][i]
@@ -151,15 +148,16 @@ def tile_moe_two_lin_relu2_kernel(tc, xT, w8_words, w8_scales, w4_words, w4_scal
         interleave(1, 2)
         quantise(1, 512, 768)
         quantise(1, 768, 1024)
-        for e0, e1 in ((0, 2), (2, 4), (4, 8)):
+        for e0, e1 in ((0, 2), (2, 5), (5, 8)):
             gather(g_scales, scales, e0, e1)
             gather(g_words[1], words[1], e0, e1)
 
-        banks = [psum.tile([P, 2, W], F32, name=f"bank{i}") for i in range(len(PIECES))]
-        relu = [keep.tile([P, 2, W], F32, name=f"relu{i}") for i in range(len(PIECES))]
-        other = [keep.tile([P, 2, W], F32, name=f"other{i}") for i in range(6)]
-        other = other + [other[5], other[5]]
-        gated = {run: keep.tile([P, 2, (run[2] - run[1]) * C], F32, name=f"gated{run[0]}_{run[1]}") for run in RUNS}
+        banks = [psum.tile([P, BANK], F32, name=f"bank{i}") for i in range(8)]
+        widths = [(e1 - e0) * C for m, e0, e1 in PIECES]
+        relu = [keep.tile([P, 2, w], F32, name=f"relu{i}") for i, w in enumerate(widths)]
+        other = [keep.tile([P, 2, w], F32, name=f"other{i}") for i, w in enumerate(widths[:LAST])]
+        other = other + [other[LAST - 1]]
+        gated = [keep.tile([P, 2, w], F32, name=f"gated{i}") for i, w in enumerate(widths)]
 
         for n in (1, 3, 0, 2):
             nc.gpsimd.tensor_copy(window[n][:, T : T + NT * E], bias[:])
@@ -169,20 +167,25 @@ def tile_moe_two_lin_relu2_kernel(tc, xT, w8_words, w8_scales, w4_words, w4_scal
                 return bias[:, n * E + e : n * E + e + 1]
             return window[holder][:, T + n * E + e : T + n * E + e + 1]
 
-        def blocks(i):
-            m, g = PIECES[i]
-            return [(h, 2 * m + h, 2 * g + d, slice(d * C, (d + 1) * C)) for d in range(2) for h in range(2)]
+        def blocks(i, halves=(0, 1)):
+            m, e0, e1 = PIECES[i]
+            if i == 0:
+                return [(h, 2 * m + h, e, e - e0) for e in range(e0, e1) for h in halves]
+            return [(h, 2 * m + h, e, e - e0) for h in halves for e in range(e0, e1)]
 
-        def sums(i, h, place):
-            bank = banks[LAST] if i == 0 and place.start else banks[i]
-            return bank[:, h, place]
+        def sums(i, h, d):
+            if i == 0:
+                return banks[d][:, h * C : (h + 1) * C]
+            if i == 1:
+                return banks[2][:, (2 * h + d) * C : (2 * h + d + 1) * C]
+            return banks[(2 * i - 1 + h) % 8][:, d * C : (d + 1) * C]
 
         def multiply(i):
-            for h, n, e, place in blocks(i):
+            for h, n, e, d in blocks(i):
                 slots = slice(e * C, (e + 1) * C)
                 w_cols = slice(e * N + n * P, e * N + (n + 1) * P)
                 nc.tensor.matmul_mx(
-                    out=sums(i, h, place),
+                    out=sums(i, h, d),
                     lhsT=w8_t[:, e, 4 * n * P : 4 * (n + 1) * P].bitcast(FP8X4),
                     lhsT_scale=w_sc[4:P, w_cols],
                     rhs=g_words[0][:, slots].bitcast(FP8X4),
@@ -191,7 +194,7 @@ def tile_moe_two_lin_relu2_kernel(tc, xT, w8_words, w8_scales, w4_words, w4_scal
                     stop=False,
                 )
                 nc.tensor.matmul_mx(
-                    out=sums(i, h, place),
+                    out=sums(i, h, d),
                     lhsT=w4_t[:, e, 2 * n * P : 2 * (n + 1) * P].bitcast(FP4X4),
                     lhsT_scale=w_sc[:, w_cols],
                     rhs=g_words[1][:, slots].bitcast(FP8X4),
@@ -200,91 +203,72 @@ def tile_moe_two_lin_relu2_kernel(tc, xT, w8_words, w8_scales, w4_words, w4_scal
                     stop=True,
                 )
 
-        def results(m, e0, e1):
-            run = [r for r in RUNS if r[0] == m and r[1] <= e0 < r[2]][0]
-            return gated[run][:, :, (e0 - run[1]) * C : (e1 - run[1]) * C]
-
-        def result(i):
-            m, g = PIECES[i]
-            return results(m, 2 * g, 2 * g + 2)
+        def held(steps, first, last):
+            return [(step, first if k == 0 else last if k == len(steps) - 1 else None) for k, step in enumerate(steps)]
 
         def gate_of(i):
-            g = PIECES[i][1]
-            return gate_t[:, g * W : (g + 1) * W]
+            m, e0, e1 = PIECES[i]
+            return gate_t[:, e0 * C : e1 * C]
 
         def gate_product(i):
-            if i == LAST:
-                nc.gpsimd.tensor_tensor(result(i)[:, 1, :], other[i][:, 1, :], gate_of(i), MULT)
-            else:
-                nc.gpsimd.tensor_tensor(result(i), other[i][:], gate_of(i).unsqueeze(1).to_broadcast([P, 2, W]), MULT)
+            nc.gpsimd.tensor_tensor(gated[i][:], other[i][:], gate_of(i).unsqueeze(1).to_broadcast([P, 2, widths[i]]), MULT)
 
-        def scalar_relu(i):
-            for h, n, e, place in blocks(i):
-                holder = 2 * h + 1 if i >= 2 else None
-                nc.scalar.activation(relu[i][:, h, place], sums(i, h, place), RELU, bias=bias_of(holder, n, e))
+        def scalar_relu(i, halves=(0, 1), first=None, last=None):
+            for (h, n, e, d), holder in held(blocks(i, halves), first, last):
+                nc.scalar.activation(relu[i][:, h, d * C : (d + 1) * C], sums(i, h, d), RELU, bias=bias_of(holder, n, e))
 
-        def vector_relu(i):
-            for h, n, e, place in blocks(i):
-                nc.vector.tensor_scalar(relu[i][:, h, place], sums(i, h, place), bias_of(2 * h, n, e), 0.0, ADD, MAX)
+        def vector_relu(i, halves, first, last):
+            for (h, n, e, d), holder in held(blocks(i, halves), first, last):
+                nc.vector.tensor_scalar(relu[i][:, h, d * C : (d + 1) * C], sums(i, h, d), bias_of(holder, n, e), 0.0, ADD, MAX)
 
-        def scalar_square(i):
-            nc.scalar.activation(other[i][:], relu[i][:], SQUARE)
-            gate_product(i)
-
-        def vector_gate(i):
-            for h, n, e, place in blocks(i):
+        def vector_gate(i, first=None, last=None):
+            for (h, n, e, d), holder in held(blocks(i), first, last):
                 nc.vector.scalar_tensor_tensor(
-                    other[i][:, h, place], sums(i, h, place), bias_of(2 * h, n, e), gate_t[:, e * C : (e + 1) * C], ADD, MULT
+                    other[i][:, h, d * C : (d + 1) * C],
+                    sums(i, h, d),
+                    bias_of(holder, n, e),
+                    gate_t[:, e * C : (e + 1) * C],
+                    ADD,
+                    MULT,
                 )
-            nc.gpsimd.tensor_tensor(result(i), other[i][:], relu[i][:], MULT)
+            nc.gpsimd.tensor_tensor(gated[i][:], other[i][:], relu[i][:], MULT)
 
-        def gpsimd_square(i):
-            nc.gpsimd.tensor_tensor(other[i][:], relu[i][:], relu[i][:], MULT)
-            gate_product(i)
+        def scatter(i):
+            m, e0, e1 = PIECES[i]
+            places = dst_t[:, 8 * e0 : 8 * e1]
+            nc.scalar.activation(window[2 * m + 1][:].indirect(places), gated[i][:, 1, :], COPY)
+            if i == LAST:
+                nc.vector.tensor_tensor(window[2 * m][:].indirect(places), other[i][:, 0, :], gate_of(i), MULT)
+            else:
+                nc.vector.tensor_copy(window[2 * m][:].indirect(places), gated[i][:, 0, :])
+            if e1 == E:
+                for n in (2 * m + 1, 2 * m):
+                    nc.sync.dma_start(out=out[n * P : (n + 1) * P, :], in_=window[n][:, 0:T])
 
-        def vector_scatter(m, e0, e1):
-            nc.vector.tensor_copy(window[2 * m][:].indirect(dst_t[:, 8 * e0 : 8 * e1]), results(m, e0, e1)[:, 0, :])
-
-        def scalar_scatter(m, e0, e1):
-            nc.scalar.activation(
-                window[2 * m + 1][:].indirect(dst_t[:, 8 * e0 : 8 * e1]), results(m, e0, e1)[:, 1, :], COPY
-            )
-
-        def store(n):
-            nc.sync.dma_start(out=out[n * P : (n + 1) * P, :], in_=window[n][:, 0:T])
-
-        for i in range(EARLY):
+        multiply(0)
+        scalar_relu(0)
+        nc.scalar.activation(other[0][:], relu[0][:], SQUARE)
+        gate_product(0)
+        for i in (1, 2):
             multiply(i)
             scalar_relu(i)
-            if i == 1:
-                vector_gate(i)
-            else:
-                scalar_square(i)
-        for i in range(EARLY, len(PIECES)):
-            multiply(i)
-        vector_scatter(0, 0, 2)
-        scalar_scatter(0, 0, 2)
-        vector_relu(4)
-        vector_gate(4)
-        scalar_relu(6)
-        vector_scatter(1, 0, 2)
-        scalar_scatter(1, 0, 2)
-        vector_relu(5)
-        vector_gate(5)
-        vector_relu(7)
-        gpsimd_square(6)
-        gpsimd_square(7)
-        vector_scatter(0, 2, 4)
-        vector_scatter(1, 2, 4)
-        scalar_scatter(1, 2, 4)
-        scalar_scatter(0, 2, 5)
-        scalar_scatter(0, 5, 8)
-        store(1)
-        vector_scatter(0, 4, 8)
-        store(0)
-        vector_scatter(1, 4, 6)
-        scalar_scatter(1, 4, 6)
-        scalar_scatter(1, 6, 8)
-        store(3)
-        nc.vector.tensor_tensor(window[2][:].indirect(dst_t[:, 48:64]), other[LAST][:, 0, :], gate_of(LAST), MULT)
-        store(2)
+            vector_gate(i)
+        multiply(3)
+        scalar_relu(3, first=1, last=3)
+        vector_gate(3, first=0, last=2)
+        multiply(4)
+        multiply(5)
+        scatter(0)
+        scalar_relu(4, (1,), 3, 1)
+        vector_relu(4, (0,), 2, 0)
+        nc.gpsimd.tensor_tensor(other[4][:], relu[4][:], relu[4][:], MULT)
+        for h in (1, 0):
+            nc.gpsimd.tensor_tensor(gated[4][:, h, :], other[4][:, h, :], gate_of(4), MULT)
+        scatter(1)
+        scalar_relu(5, (1,), 1, 3)
+        vector_relu(5, (0,), 0, 2)
+        nc.gpsimd.tensor_tensor(other[5][:, 0, :], relu[5][:, 1, :], relu[5][:, 1, :], MULT)
+        nc.gpsimd.tensor_tensor(gated[5][:, 1, :], other[5][:, 0, :], gate_of(5), MULT)
+        nc.gpsimd.tensor_tensor(other[5][:, 0, :], relu[5][:, 0, :], relu[5][:, 0, :], MULT)
+        for i in range(2, len(PIECES)):
+            scatter(i)

@@ -1,4 +1,5 @@
 import concourse.mybir as mybir
+from concourse.masks import make_identity
 
 K, T, E, C, N = 1024, 1024, 8, 128, 512
 P = 128
@@ -39,6 +40,9 @@ def tile_moe_two_lin_relu2_kernel(tc, xT, w8_words, w8_scales, w4_words, w4_scal
         offs_t = keep.tile([P, 64], U16, name="offs_t")
         dst_t = keep.tile([P, 64], U16, name="dst_t")
         gate_t = keep.tile([P, T], F32, name="gate_t")
+        gate_row = keep.tile([P, E], F32, name="gate_row")
+        identity = keep.tile([P, P], F32, name="identity")
+        banks = [psum.tile([P, BANK], F32, name=f"bank{i}") for i in range(8)]
         words = [keep.tile([P, 2 * T if a == 0 else T], U32, name=f"words{a}", align_bytes=256) for a in range(2)]
         scales = keep.tile([P, T], U8, name="scales", align_bytes=256)
         g_words = [keep.tile([P, T], U32, name=f"g_words{a}", align_bytes=256) for a in range(2)]
@@ -63,16 +67,14 @@ def tile_moe_two_lin_relu2_kernel(tc, xT, w8_words, w8_scales, w4_words, w4_scal
                 out=w4_t[:, e0:e1, :].bitcast(I32), in_=w4_words[e0:e1].rearrange("e a p n -> (a p) e n").bitcast(I32)
             )
 
-        def load_scales(i):
+        def load_scales(i, e0, e1):
             plane, sc = ((0, w4_scales), (4, w8_scales))[i % 2]
             nc.sync.dma_start(
-                out=w_sc[plane + i // 2 : P : 32, :].bitcast(I32).rearrange("q (e n) -> q e n", e=E),
-                in_=sc.bitcast(I32).rearrange("e a (q r) n -> r a q e n", r=4)[i // 2][0],
+                out=w_sc[plane + i // 2 : P : 32, :].bitcast(I32).rearrange("q (e n) -> q e n", e=E)[:, e0:e1, :],
+                in_=sc.bitcast(I32).rearrange("e a (q r) n -> r a q e n", r=4)[i // 2][0][:, e0:e1, :],
             )
 
-        def load_gate(e0, e1):
-            nc.sync.dma_start(out=gate_t[:, e0 * C : e1 * C], in_=gate[0:P, e0 * C : e1 * C])
-
+        nc.sync.dma_start(out=gate_row[:], in_=gate[0].rearrange("(p j) -> p j", j=E))
         x_view = xT.rearrange("(a p j) t -> a p j t", a=2, j=J)
         raws = {}
         grouped = [keep.tile([P, T * J], BF16, name=f"grouped{a}", align_bytes=256) for a in range(2)]
@@ -85,19 +87,20 @@ def tile_moe_two_lin_relu2_kernel(tc, xT, w8_words, w8_scales, w4_words, w4_scal
                     nc.sync.dma_start(out=bias[:].rearrange("p (n e) -> p n e", e=E), in_=b.rearrange("(n p) e -> p n e", p=P))
 
         for i in range(5):
-            load_scales(i)
+            load_scales(i, 0, 5)
         load_w8(0, 2)
         load_w4(0, 2)
         for i in range(5, 8):
-            load_scales(i)
+            load_scales(i, 0, 5)
         load_w8(2, 5)
-        load_gate(0, 2)
         load_w4(2, 5)
         nc.sync.dma_start(dst_t[:], dst)
-        load_gate(2, 5)
+        for i in range(5):
+            load_scales(i, 5, 8)
         load_w8(5, 8)
         load_w4(5, 8)
-        load_gate(5, 8)
+        for i in range(5, 8):
+            load_scales(i, 5, 8)
 
         def round_tokens(copy, a, i, lo, hi):
             t0, width, j0, rows, v = CHUNKS[a][i]
@@ -152,12 +155,22 @@ def tile_moe_two_lin_relu2_kernel(tc, xT, w8_words, w8_scales, w4_words, w4_scal
             gather(g_scales, scales, e0, e1)
             gather(g_words[1], words[1], e0, e1)
 
-        banks = [psum.tile([P, BANK], F32, name=f"bank{i}") for i in range(8)]
         widths = [(e1 - e0) * C for m, e0, e1 in PIECES]
         relu = [keep.tile([P, 2, w], F32, name=f"relu{i}") for i, w in enumerate(widths)]
         other = [keep.tile([P, 2, w], F32, name=f"other{i}") for i, w in enumerate(widths[:LAST])]
         other = other + [other[LAST - 1]]
         gated = [keep.tile([P, 2, w], F32, name=f"gated{i}") for i, w in enumerate(widths)]
+
+        make_identity(nc, identity[:])
+        for half in range(2):
+            bank = banks[6 + half]
+            for j in range(J):
+                column = gate_row[:, J * half + j : J * half + j + 1]
+                nc.tensor.transpose(bank[:, j * P : (j + 1) * P], column.to_broadcast([P, P]), identity[:])
+            nc.scalar.copy(
+                out=gate_t[:].rearrange("q (p j) -> q p j", j=E)[:, :, J * half : J * (half + 1)],
+                in_=bank[:].rearrange("q (j p) -> q p j", j=J),
+            )
 
         for n in (1, 3, 0, 2):
             nc.gpsimd.tensor_copy(window[n][:, T : T + NT * E], bias[:])
@@ -259,12 +272,12 @@ def tile_moe_two_lin_relu2_kernel(tc, xT, w8_words, w8_scales, w4_words, w4_scal
         multiply(4)
         multiply(5)
         scatter(0)
-        scalar_relu(4, (1,), 3, 1)
         vector_relu(4, (0,), 2, 0)
+        scatter(1)
+        scalar_relu(4, (1,), 1, None)
         nc.gpsimd.tensor_tensor(other[4][:], relu[4][:], relu[4][:], MULT)
         for h in (1, 0):
             nc.gpsimd.tensor_tensor(gated[4][:, h, :], other[4][:, h, :], gate_of(4), MULT)
-        scatter(1)
         scalar_relu(5, (1,), 1, 3)
         vector_relu(5, (0,), 0, 2)
         nc.gpsimd.tensor_tensor(other[5][:, 0, :], relu[5][:, 1, :], relu[5][:, 1, :], MULT)

@@ -47,8 +47,8 @@ def tile_moe_two_lin_relu2_kernel(tc, xT, w8_words, w8_scales, w4_words, w4_scal
         scales = keep.tile([P, T], U8, name="scales", align_bytes=256)
         g_words = [keep.tile([P, T], U32, name=f"g_words{a}", align_bytes=256) for a in range(2)]
         g_scales = keep.tile([P, T], U8, name="g_scales", align_bytes=256)
-        w8_t = keep.tile([P, E, 4 * N], U8, name="w8_t", align_bytes=256)
-        w4_t = keep.tile([P, E, 2 * N], U8, name="w4_t", align_bytes=256)
+        w8_t = {}
+        w4_t = {}
         w_sc = keep.tile([P, E * N], U8, name="w_sc", align_bytes=256)
         window = [keep.tile([P, T + NT * E], F32, name=f"window{n}") for n in range(NT)]
         bias = keep.tile([P, NT * E], F32, name="bias")
@@ -56,16 +56,16 @@ def tile_moe_two_lin_relu2_kernel(tc, xT, w8_words, w8_scales, w4_words, w4_scal
         nc.gpsimd.memset(scales[:], 0)
         nc.vector.memset(w_sc[:].bitcast(I32), 0)
 
-        def load_w8(e0, e1):
-            nc.sync.dma_start(
-                out=w8_t[:, e0:e1, :].bitcast(I32),
-                in_=w8_words[e0:e1].rearrange("e a p n r -> (a p) e (n r)").bitcast(I32),
-            )
-
-        def load_w4(e0, e1):
-            nc.sync.dma_start(
-                out=w4_t[:, e0:e1, :].bitcast(I32), in_=w4_words[e0:e1].rearrange("e a p n -> (a p) e n").bitcast(I32)
-            )
+        def load_words(e0, e1, n0, n1):
+            for held_in, source, size in (
+                (w8_t, w8_words.rearrange("e a p n r -> (a p) e (n r)"), 4),
+                (w4_t, w4_words.rearrange("e a p n -> (a p) e n"), 2),
+            ):
+                tile = keep.tile([P, e1 - e0, size * (n1 - n0)], U8, name=f"w{size}_{e0}_{n0}", align_bytes=256)
+                nc.sync.dma_start(out=tile[:].bitcast(I32), in_=source[:, e0:e1, size * n0 : size * n1].bitcast(I32))
+                for e in range(e0, e1):
+                    for n in range(n0 // P, n1 // P):
+                        held_in[e, n] = tile[:, e - e0, size * (n * P - n0) : size * ((n + 1) * P - n0)]
 
         def load_scales(i, e0, e1):
             plane, sc = ((0, w4_scales), (4, w8_scales))[i % 2]
@@ -88,19 +88,18 @@ def tile_moe_two_lin_relu2_kernel(tc, xT, w8_words, w8_scales, w4_words, w4_scal
 
         for i in range(5):
             load_scales(i, 0, 5)
-        load_w8(0, 2)
-        load_w4(0, 2)
+        load_words(0, 2, 0, N)
         for i in range(5, 8):
             load_scales(i, 0, 5)
-        load_w8(2, 5)
-        load_w4(2, 5)
+        for n0 in (0, N // 2):
+            load_words(2, 5, n0, n0 + N // 2)
         nc.sync.dma_start(dst_t[:], dst)
-        for i in range(5):
+        for i in range(3):
             load_scales(i, 5, 8)
-        load_w8(5, 8)
-        load_w4(5, 8)
-        for i in range(5, 8):
+        load_words(5, 8, 0, N // 2)
+        for i in range(3, 8):
             load_scales(i, 5, 8)
+        load_words(5, 8, N // 2, N)
 
         def round_tokens(copy, a, i, lo, hi):
             t0, width, j0, rows, v = CHUNKS[a][i]
@@ -158,8 +157,9 @@ def tile_moe_two_lin_relu2_kernel(tc, xT, w8_words, w8_scales, w4_words, w4_scal
         widths = [(e1 - e0) * C for m, e0, e1 in PIECES]
         relu = [keep.tile([P, 2, w], F32, name=f"relu{i}") for i, w in enumerate(widths)]
         other = [keep.tile([P, 2, w], F32, name=f"other{i}") for i, w in enumerate(widths[:LAST])]
-        other = other + [other[LAST - 1]]
         gated = [keep.tile([P, 2, w], F32, name=f"gated{i}") for i, w in enumerate(widths)]
+        result = [[gated[i][:, h, :] for h in range(2)] for i in range(LAST - 1)]
+        result = result + [[relu[LAST][:, 1, :], gated[LAST - 1][:, 1, :]], [other[LAST - 1][:, 0, :], gated[LAST][:, 1, :]]]
 
         make_identity(nc, identity[:])
         for half in range(2):
@@ -173,7 +173,7 @@ def tile_moe_two_lin_relu2_kernel(tc, xT, w8_words, w8_scales, w4_words, w4_scal
             )
 
         for n in (1, 3, 0, 2):
-            nc.gpsimd.tensor_copy(window[n][:, T : T + NT * E], bias[:])
+            nc.scalar.copy(out=window[n][:, T : T + NT * E], in_=bias[:])
 
         def bias_of(holder, n, e):
             if holder is None:
@@ -199,7 +199,7 @@ def tile_moe_two_lin_relu2_kernel(tc, xT, w8_words, w8_scales, w4_words, w4_scal
                 w_cols = slice(e * N + n * P, e * N + (n + 1) * P)
                 nc.tensor.matmul_mx(
                     out=sums(i, h, d),
-                    lhsT=w8_t[:, e, 4 * n * P : 4 * (n + 1) * P].bitcast(FP8X4),
+                    lhsT=w8_t[e, n].bitcast(FP8X4),
                     lhsT_scale=w_sc[4:P, w_cols],
                     rhs=g_words[0][:, slots].bitcast(FP8X4),
                     rhs_scale=g_scales[4:P, slots],
@@ -208,7 +208,7 @@ def tile_moe_two_lin_relu2_kernel(tc, xT, w8_words, w8_scales, w4_words, w4_scal
                 )
                 nc.tensor.matmul_mx(
                     out=sums(i, h, d),
-                    lhsT=w4_t[:, e, 2 * n * P : 2 * (n + 1) * P].bitcast(FP4X4),
+                    lhsT=w4_t[e, n].bitcast(FP4X4),
                     lhsT_scale=w_sc[:, w_cols],
                     rhs=g_words[1][:, slots].bitcast(FP8X4),
                     rhs_scale=g_scales[:, slots],
@@ -249,14 +249,15 @@ def tile_moe_two_lin_relu2_kernel(tc, xT, w8_words, w8_scales, w4_words, w4_scal
         def scatter(i):
             m, e0, e1 = PIECES[i]
             places = dst_t[:, 8 * e0 : 8 * e1]
-            nc.scalar.activation(window[2 * m + 1][:].indirect(places), gated[i][:, 1, :], COPY)
+            nc.scalar.activation(window[2 * m + 1][:].indirect(places), result[i][1], COPY)
             if i == LAST:
-                nc.vector.tensor_tensor(window[2 * m][:].indirect(places), other[i][:, 0, :], gate_of(i), MULT)
+                nc.vector.tensor_tensor(window[2 * m][:].indirect(places), result[i][0], gate_of(i), MULT)
             else:
-                nc.vector.tensor_copy(window[2 * m][:].indirect(places), gated[i][:, 0, :])
+                nc.vector.tensor_copy(window[2 * m][:].indirect(places), result[i][0])
             if e1 == E:
                 for n in (2 * m + 1, 2 * m):
-                    nc.sync.dma_start(out=out[n * P : (n + 1) * P, :], in_=window[n][:, 0:T])
+                    queue = nc.scalar if n == NT - 1 else nc.sync
+                    queue.dma_start(out=out[n * P : (n + 1) * P, :], in_=window[n][:, 0:T])
 
         multiply(0)
         scalar_relu(0)
@@ -276,12 +277,12 @@ def tile_moe_two_lin_relu2_kernel(tc, xT, w8_words, w8_scales, w4_words, w4_scal
         scatter(1)
         scalar_relu(4, (1,), 1, None)
         nc.gpsimd.tensor_tensor(other[4][:], relu[4][:], relu[4][:], MULT)
-        for h in (1, 0):
-            nc.gpsimd.tensor_tensor(gated[4][:, h, :], other[4][:, h, :], gate_of(4), MULT)
+        nc.gpsimd.tensor_tensor(result[4][1], other[4][:, 1, :], gate_of(4), MULT)
         scalar_relu(5, (1,), 1, 3)
         vector_relu(5, (0,), 0, 2)
-        nc.gpsimd.tensor_tensor(other[5][:, 0, :], relu[5][:, 1, :], relu[5][:, 1, :], MULT)
-        nc.gpsimd.tensor_tensor(gated[5][:, 1, :], other[5][:, 0, :], gate_of(5), MULT)
-        nc.gpsimd.tensor_tensor(other[5][:, 0, :], relu[5][:, 0, :], relu[5][:, 0, :], MULT)
+        nc.gpsimd.tensor_tensor(other[4][:, 1, :], relu[5][:, 1, :], relu[5][:, 1, :], MULT)
+        nc.gpsimd.tensor_tensor(result[4][0], other[4][:, 0, :], gate_of(4), MULT)
+        nc.gpsimd.tensor_tensor(result[5][1], other[4][:, 1, :], gate_of(5), MULT)
+        nc.gpsimd.tensor_tensor(result[5][0], relu[5][:, 0, :], relu[5][:, 0, :], MULT)
         for i in range(2, len(PIECES)):
             scatter(i)

@@ -256,8 +256,7 @@ def tile_moe_two_lin_relu2_kernel(tc, xT, w8_words, w8_scales, w4_words, w4_scal
                 nc.vector.tensor_copy(window[2 * m][:].indirect(places), result[i][0])
             if e1 == E:
                 for n in (2 * m + 1, 2 * m):
-                    queue = nc.scalar if n == NT - 1 else nc.sync
-                    queue.dma_start(out=out[n * P : (n + 1) * P, :], in_=window[n][:, 0:T])
+                    nc.sync.dma_start(out=out[n * P : (n + 1) * P, :], in_=window[n][:, 0:T])
 
         multiply(0)
         scalar_relu(0)
@@ -273,9 +272,9 @@ def tile_moe_two_lin_relu2_kernel(tc, xT, w8_words, w8_scales, w4_words, w4_scal
         multiply(4)
         multiply(5)
         scatter(0)
-        vector_relu(4, (0,), 2, 0)
+        vector_relu(4, (0,), None, None)
+        vector_relu(4, (1,), 2, 0)
         scatter(1)
-        scalar_relu(4, (1,), 1, None)
         nc.gpsimd.tensor_tensor(other[4][:], relu[4][:], relu[4][:], MULT)
         nc.gpsimd.tensor_tensor(result[4][1], other[4][:, 1, :], gate_of(4), MULT)
         scalar_relu(5, (1,), 1, 3)

@@ -84,11 +84,11 @@ def tile_moe_two_lin_relu2_kernel(tc, xT, w8_words, w8_scales, w4_words, w4_scal
                 nc.sync.dma_start(out=raws[a, i][:], in_=x_view[a][:, j0 : j0 + rows, t0 : t0 + width])
                 if (a, i) == (0, 2):
                     nc.sync.dma_start(offs_t[:], offs)
-                    nc.sync.dma_start(out=bias[:].rearrange("p (n e) -> p n e", e=E), in_=b.rearrange("(n p) e -> p n e", p=P))
 
         for i in range(5):
             load_scales(i, 0, 5)
         load_words(0, 2, 0, N)
+        nc.sync.dma_start(out=bias[:].rearrange("p (n e) -> p n e", e=E), in_=b.rearrange("(n p) e -> p n e", p=P))
         for i in range(5, 8):
             load_scales(i, 0, 5)
         for n0 in (0, N // 2):

@@ -31,6 +31,7 @@ CHUNKS = (
 PLANE = (4, 0)
 PIECES = tuple((m, e0, e1) for e0, e1 in ((0, 2), (2, 5), (5, 8)) for m in range(2))
 LAST = len(PIECES) - 1
+GROUPS = ((0, 2), (2, 5), (5, 8))
 BANK = 512
 
 
@@ -49,57 +50,66 @@ def tile_moe_two_lin_relu2_kernel(tc, xT, w8_words, w8_scales, w4_words, w4_scal
         g_scales = keep.tile([P, T], U8, name="g_scales", align_bytes=256)
         w8_t = {}
         w4_t = {}
-        w_sc = keep.tile([P, E * N], U8, name="w_sc", align_bytes=256)
-        window = [keep.tile([P, T + NT * E], F32, name=f"window{n}") for n in range(NT)]
+        w_sc = [keep.tile([P, (e1 - e0) * N], U8, name=f"w_sc{e0}", align_bytes=256) for e0, e1 in GROUPS]
+        window = [keep.tile([P, T + NT * E], F32, name=f"window{n}", align_bytes=256) for n in range(NT)]
         bias = keep.tile([P, NT * E], F32, name="bias")
 
         nc.gpsimd.memset(scales[:], 0)
-        nc.vector.memset(w_sc[:].bitcast(I32), 0)
+        for plane_tile in w_sc:
+            nc.vector.memset(plane_tile[:].bitcast(I32), 0)
 
-        def load_words(e0, e1, n0, n1):
-            for held_in, source, size in (
+        def load_words(which, e0, e1, n0, n1):
+            held_in, source, size = (
                 (w8_t, w8_words.rearrange("e a p n r -> (a p) e (n r)"), 4),
                 (w4_t, w4_words.rearrange("e a p n -> (a p) e n"), 2),
-            ):
-                tile = keep.tile([P, e1 - e0, size * (n1 - n0)], U8, name=f"w{size}_{e0}_{n0}", align_bytes=256)
-                nc.sync.dma_start(out=tile[:].bitcast(I32), in_=source[:, e0:e1, size * n0 : size * n1].bitcast(I32))
-                for e in range(e0, e1):
-                    for n in range(n0 // P, n1 // P):
-                        held_in[e, n] = tile[:, e - e0, size * (n * P - n0) : size * ((n + 1) * P - n0)]
+            )[which]
+            tile = keep.tile([P, e1 - e0, size * (n1 - n0)], U8, name=f"w{size}_{e0}_{n0}", align_bytes=256)
+            nc.sync.dma_start(out=tile[:].bitcast(I32), in_=source[:, e0:e1, size * n0 : size * n1].bitcast(I32))
+            for e in range(e0, e1):
+                for n in range(n0 // P, n1 // P):
+                    held_in[e, n] = tile[:, e - e0, size * (n * P - n0) : size * ((n + 1) * P - n0)]
 
-        def load_scales(i, e0, e1):
-            plane, sc = ((0, w4_scales), (4, w8_scales))[i % 2]
-            nc.sync.dma_start(
-                out=w_sc[plane + i // 2 : P : 32, :].bitcast(I32).rearrange("q (e n) -> q e n", e=E)[:, e0:e1, :],
-                in_=sc.bitcast(I32).rearrange("e a (q r) n -> r a q e n", r=4)[i // 2][0][:, e0:e1, :],
-            )
+        def load_scales(run, i0, i1):
+            e0, e1 = GROUPS[run]
+            for i in range(i0, i1):
+                plane, sc = ((0, w4_scales), (4, w8_scales))[i % 2]
+                nc.sync.dma_start(
+                    out=w_sc[run][plane + i // 2 : P : 32, :].bitcast(I32).rearrange("q (e n) -> q e n", e=e1 - e0),
+                    in_=sc.bitcast(I32).rearrange("e a (q r) n -> r a q e n", r=4)[i // 2][0][:, e0:e1, :],
+                )
 
-        nc.sync.dma_start(out=gate_row[:], in_=gate[0].rearrange("(p j) -> p j", j=E))
         x_view = xT.rearrange("(a p j) t -> a p j t", a=2, j=J)
         raws = {}
         grouped = [keep.tile([P, T * J], BF16, name=f"grouped{a}", align_bytes=256) for a in range(2)]
-        for a in range(2):
-            for i, (t0, width, j0, rows, v) in enumerate(CHUNKS[a]):
-                raws[a, i] = keep.tile([P, rows, width], F32, name=f"raw{a}_{i}")
-                nc.sync.dma_start(out=raws[a, i][:], in_=x_view[a][:, j0 : j0 + rows, t0 : t0 + width])
-                if (a, i) == (0, 2):
-                    nc.sync.dma_start(offs_t[:], offs)
 
-        for i in range(5):
-            load_scales(i, 0, 5)
-        load_words(0, 2, 0, N)
-        nc.sync.dma_start(out=bias[:].rearrange("p (n e) -> p n e", e=E), in_=b.rearrange("(n p) e -> p n e", p=P))
-        for i in range(5, 8):
-            load_scales(i, 0, 5)
-        for n0 in (0, N // 2):
-            load_words(2, 5, n0, n0 + N // 2)
-        nc.sync.dma_start(dst_t[:], dst)
+        def load_tokens(a, i):
+            t0, width, j0, rows, v = CHUNKS[a][i]
+            raws[a, i] = keep.tile([P, rows, width], F32, name=f"raw{a}_{i}", align_bytes=256)
+            nc.sync.dma_start(out=raws[a, i][:], in_=x_view[a][:, j0 : j0 + rows, t0 : t0 + width])
+
+        nc.sync.dma_start(out=gate_row[:], in_=gate[0].rearrange("(p j) -> p j", j=E))
         for i in range(3):
-            load_scales(i, 5, 8)
-        load_words(5, 8, 0, N // 2)
-        for i in range(3, 8):
-            load_scales(i, 5, 8)
-        load_words(5, 8, N // 2, N)
+            load_tokens(0, i)
+        nc.sync.dma_start(offs_t[:], offs)
+        load_tokens(1, 0)
+        load_scales(0, 0, 3)
+        load_tokens(1, 1)
+        load_tokens(1, 2)
+        load_scales(0, 3, 8)
+        load_words(0, 0, 2, 0, N)
+        load_words(1, 0, 2, 0, N)
+        nc.sync.dma_start(out=bias[:].rearrange("p (n e) -> p n e", e=E), in_=b.rearrange("(n p) e -> p n e", p=P))
+        for g in (1, 2):
+            e0, e1 = GROUPS[g]
+            load_scales(g, 0, 3)
+            load_words(0, e0, e1, 0, N // 2)
+            load_scales(g, 3, 5)
+            load_words(1, e0, e1, 0, N // 2)
+            load_scales(g, 5, 8)
+            load_words(0, e0, e1, N // 2, N)
+            load_words(1, e0, e1, N // 2, N)
+            if g == 1:
+                nc.sync.dma_start(dst_t[:], dst)
 
         def round_tokens(copy, a, i, lo, hi):
             t0, width, j0, rows, v = CHUNKS[a][i]
@@ -196,11 +206,12 @@ def tile_moe_two_lin_relu2_kernel(tc, xT, w8_words, w8_scales, w4_words, w4_scal
         def multiply(i):
             for h, n, e, d in blocks(i):
                 slots = slice(e * C, (e + 1) * C)
-                w_cols = slice(e * N + n * P, e * N + (n + 1) * P)
+                first = (e - GROUPS[i // 2][0]) * N + n * P
+                w_cols = slice(first, first + P)
                 nc.tensor.matmul_mx(
                     out=sums(i, h, d),
                     lhsT=w8_t[e, n].bitcast(FP8X4),
-                    lhsT_scale=w_sc[4:P, w_cols],
+                    lhsT_scale=w_sc[i // 2][4:P, w_cols],
                     rhs=g_words[0][:, slots].bitcast(FP8X4),
                     rhs_scale=g_scales[4:P, slots],
                     start=True,
@@ -209,7 +220,7 @@ def tile_moe_two_lin_relu2_kernel(tc, xT, w8_words, w8_scales, w4_words, w4_scal
                 nc.tensor.matmul_mx(
                     out=sums(i, h, d),
                     lhsT=w4_t[e, n].bitcast(FP4X4),
-                    lhsT_scale=w_sc[:, w_cols],
+                    lhsT_scale=w_sc[i // 2][:, w_cols],
                     rhs=g_words[1][:, slots].bitcast(FP8X4),
                     rhs_scale=g_scales[:, slots],
                     start=False,

@@ -26,7 +26,7 @@ NT = N // P
 HALF = T // 2
 CHUNKS = (
     ((0, 1024, 0, 2, 0), (0, 512, 2, 2, 336), (512, 512, 2, 2, 336)),
-    ((0, 512, 0, 4, 0), (512, 256, 0, 4, 0), (768, 256, 0, 4, 160)),
+    ((0, 512, 0, 4, 0), (512, 256, 0, 4, 0), (768, 256, 0, 4, 184)),
 )
 PLANE = (4, 0)
 PIECES = tuple((m, e0, e1) for e0, e1 in ((0, 2), (2, 5), (5, 8)) for m in range(2))
@@ -40,7 +40,6 @@ def tile_moe_two_lin_relu2_kernel(tc, xT, w8_words, w8_scales, w4_words, w4_scal
     with tc.tile_pool(name="keep", bufs=1) as keep, tc.psum_pool(name="psum", bufs=1) as psum:
         offs_t = keep.tile([P, 64], U16, name="offs_t")
         dst_t = keep.tile([P, 64], U16, name="dst_t")
-        gate_t = keep.tile([P, T], F32, name="gate_t")
         gate_row = keep.tile([P, E], F32, name="gate_row")
         identity = keep.tile([P, P], F32, name="identity")
         banks = [psum.tile([P, BANK], F32, name=f"bank{i}") for i in range(8)]
@@ -72,10 +71,10 @@ def tile_moe_two_lin_relu2_kernel(tc, xT, w8_words, w8_scales, w4_words, w4_scal
         def load_scales(run, i0, i1):
             e0, e1 = GROUPS[run]
             for i in range(i0, i1):
-                plane, sc = ((0, w4_scales), (4, w8_scales))[i % 2]
+                a, r = divmod(i, 4)
                 nc.sync.dma_start(
-                    out=w_sc[run][plane + i // 2 : P : 32, :].bitcast(I32).rearrange("q (e n) -> q e n", e=e1 - e0),
-                    in_=sc.bitcast(I32).rearrange("e a (q r) n -> r a q e n", r=4)[i // 2][0][:, e0:e1, :],
+                    out=w_sc[run][PLANE[a] + r : P : 32, :].bitcast(I32).rearrange("q (e n) -> q e n", e=e1 - e0),
+                    in_=(w8_scales, w4_scales)[a].bitcast(I32).rearrange("e a (q r) n -> r a q e n", r=4)[r][0][:, e0:e1, :],
                 )
 
         x_view = xT.rearrange("(a p j) t -> a p j t", a=2, j=J)
@@ -84,21 +83,21 @@ def tile_moe_two_lin_relu2_kernel(tc, xT, w8_words, w8_scales, w4_words, w4_scal
 
         def load_tokens(a, i):
             t0, width, j0, rows, v = CHUNKS[a][i]
-            raws[a, i] = keep.tile([P, rows, width], F32, name=f"raw{a}_{i}", align_bytes=256)
+            raws[a, i] = keep.tile([P, rows, width], F32, name=f"raw{a}_{i}", tag=f"raw{a}_{i}", align_bytes=256)
             nc.sync.dma_start(out=raws[a, i][:], in_=x_view[a][:, j0 : j0 + rows, t0 : t0 + width])
 
-        nc.sync.dma_start(out=gate_row[:], in_=gate[0].rearrange("(p j) -> p j", j=E))
         for i in range(3):
             load_tokens(0, i)
         nc.sync.dma_start(offs_t[:], offs)
+        nc.sync.dma_start(out=gate_row[:], in_=gate[0].rearrange("(p j) -> p j", j=E))
         load_tokens(1, 0)
-        load_scales(0, 0, 3)
+        load_scales(0, 0, 4)
         load_tokens(1, 1)
         load_tokens(1, 2)
-        load_scales(0, 3, 8)
+        load_scales(0, 4, 8)
+        nc.sync.dma_start(out=bias[:].rearrange("p (n e) -> p n e", e=E), in_=b.rearrange("(n p) e -> p n e", p=P))
         load_words(0, 0, 2, 0, N)
         load_words(1, 0, 2, 0, N)
-        nc.sync.dma_start(out=bias[:].rearrange("p (n e) -> p n e", e=E), in_=b.rearrange("(n p) e -> p n e", p=P))
         for g in (1, 2):
             e0, e1 = GROUPS[g]
             load_scales(g, 0, 3)
@@ -160,17 +159,22 @@ def tile_moe_two_lin_relu2_kernel(tc, xT, w8_words, w8_scales, w4_words, w4_scal
         interleave(1, 2)
         quantise(1, 512, 768)
         quantise(1, 768, 1024)
-        for e0, e1 in ((0, 2), (2, 5), (5, 8)):
+        for e0, e1 in ((0, 1), (1, 2), (2, 5), (5, 8)):
             gather(g_scales, scales, e0, e1)
             gather(g_words[1], words[1], e0, e1)
 
         widths = [(e1 - e0) * C for m, e0, e1 in PIECES]
-        relu = [keep.tile([P, 2, w], F32, name=f"relu{i}") for i, w in enumerate(widths)]
-        other = [keep.tile([P, 2, w], F32, name=f"other{i}") for i, w in enumerate(widths[:LAST])]
-        gated = [keep.tile([P, 2, w], F32, name=f"gated{i}") for i, w in enumerate(widths)]
-        result = [[gated[i][:, h, :] for h in range(2)] for i in range(LAST - 1)]
+        first_relu, first_square, first_gated = (
+            keep.tile([P, NT, 2 * C], F32, name=f"first_{kind}") for kind in ("relu", "square", "gated")
+        )
+        relu = {i: keep.tile([P, 2, widths[i]], F32, name=f"relu{i}") for i in range(2, LAST + 1)}
+        other = {i: keep.tile([P, 2, widths[i]], F32, name=f"other{i}") for i in range(2, LAST)}
+        gated = {i: keep.tile([P, 2, widths[i]], F32, name=f"gated{i}") for i in range(2, LAST + 1)}
+        result = [[first_gated[:, 2 * i + h, :] for h in range(2)] for i in range(2)]
+        result = result + [[gated[i][:, h, :] for h in range(2)] for i in range(2, LAST - 1)]
         result = result + [[relu[LAST][:, 1, :], gated[LAST - 1][:, 1, :]], [other[LAST - 1][:, 0, :], gated[LAST][:, 1, :]]]
 
+        gate_t = keep.tile([P, T], F32, name="gate_t", tag="raw1_2", align_bytes=256)
         make_identity(nc, identity[:])
         for half in range(2):
             bank = banks[6 + half]
@@ -182,9 +186,6 @@ def tile_moe_two_lin_relu2_kernel(tc, xT, w8_words, w8_scales, w4_words, w4_scal
                 in_=bank[:].rearrange("q (j p) -> q p j", j=J),
             )
 
-        for n in (1, 3, 0, 2):
-            nc.scalar.copy(out=window[n][:, T : T + NT * E], in_=bias[:])
-
         def bias_of(holder, n, e):
             if holder is None:
                 return bias[:, n * E + e : n * E + e + 1]
@@ -192,40 +193,33 @@ def tile_moe_two_lin_relu2_kernel(tc, xT, w8_words, w8_scales, w4_words, w4_scal
 
         def blocks(i, halves=(0, 1)):
             m, e0, e1 = PIECES[i]
-            if i == 0:
-                return [(h, 2 * m + h, e, e - e0) for e in range(e0, e1) for h in halves]
             return [(h, 2 * m + h, e, e - e0) for h in halves for e in range(e0, e1)]
 
         def sums(i, h, d):
-            if i == 0:
-                return banks[d][:, h * C : (h + 1) * C]
-            if i == 1:
-                return banks[2][:, (2 * h + d) * C : (2 * h + d + 1) * C]
-            return banks[(2 * i - 1 + h) % 8][:, d * C : (d + 1) * C]
+            return banks[(2 * i + 2 + h) % 8][:, d * C : (d + 1) * C]
+
+        def first_sums(e, n):
+            if e == 0:
+                return banks[n][:, 0:C]
+            return banks[4 + n // 2][:, (n % 2) * C : (n % 2 + 1) * C]
+
+        def one_pass(into, a, g, e, n):
+            slots = slice(e * C, (e + 1) * C)
+            first = (e - GROUPS[g][0]) * N + n * P
+            nc.tensor.matmul_mx(
+                out=into,
+                lhsT=(w8_t[e, n].bitcast(FP8X4), w4_t[e, n].bitcast(FP4X4))[a],
+                lhsT_scale=w_sc[g][PLANE[a] : P, first : first + P],
+                rhs=g_words[a][:, slots].bitcast(FP8X4),
+                rhs_scale=g_scales[PLANE[a] : P, slots],
+                start=a == 0,
+                stop=a == 1,
+            )
 
         def multiply(i):
             for h, n, e, d in blocks(i):
-                slots = slice(e * C, (e + 1) * C)
-                first = (e - GROUPS[i // 2][0]) * N + n * P
-                w_cols = slice(first, first + P)
-                nc.tensor.matmul_mx(
-                    out=sums(i, h, d),
-                    lhsT=w8_t[e, n].bitcast(FP8X4),
-                    lhsT_scale=w_sc[i // 2][4:P, w_cols],
-                    rhs=g_words[0][:, slots].bitcast(FP8X4),
-                    rhs_scale=g_scales[4:P, slots],
-                    start=True,
-                    stop=False,
-                )
-                nc.tensor.matmul_mx(
-                    out=sums(i, h, d),
-                    lhsT=w4_t[e, n].bitcast(FP4X4),
-                    lhsT_scale=w_sc[i // 2][:, w_cols],
-                    rhs=g_words[1][:, slots].bitcast(FP8X4),
-                    rhs_scale=g_scales[:, slots],
-                    start=False,
-                    stop=True,
-                )
+                for a in range(2):
+                    one_pass(sums(i, h, d), a, i // 2, e, n)
 
         def held(steps, first, last):
             return [(step, first if k == 0 else last if k == len(steps) - 1 else None) for k, step in enumerate(steps)]
@@ -233,9 +227,6 @@ def tile_moe_two_lin_relu2_kernel(tc, xT, w8_words, w8_scales, w4_words, w4_scal
         def gate_of(i):
             m, e0, e1 = PIECES[i]
             return gate_t[:, e0 * C : e1 * C]
-
-        def gate_product(i):
-            nc.gpsimd.tensor_tensor(gated[i][:], other[i][:], gate_of(i).unsqueeze(1).to_broadcast([P, 2, widths[i]]), MULT)
 
         def scalar_relu(i, halves=(0, 1), first=None, last=None):
             for (h, n, e, d), holder in held(blocks(i, halves), first, last):
@@ -269,14 +260,33 @@ def tile_moe_two_lin_relu2_kernel(tc, xT, w8_words, w8_scales, w4_words, w4_scal
                 for n in (2 * m + 1, 2 * m):
                     nc.sync.dma_start(out=out[n * P : (n + 1) * P, :], in_=window[n][:, 0:T])
 
-        multiply(0)
-        scalar_relu(0)
-        nc.scalar.activation(other[0][:], relu[0][:], SQUARE)
-        gate_product(0)
-        for i in (1, 2):
-            multiply(i)
-            scalar_relu(i)
-            vector_gate(i)
+        for a in range(2):
+            for n in range(2):
+                one_pass(first_sums(0, n), a, 0, 0, n)
+        for e, n in ((0, 2), (0, 3), (1, 0), (1, 1), (1, 2), (1, 3)):
+            for a in range(2):
+                one_pass(first_sums(e, n), a, 0, e, n)
+        for e, squared in ((0, NT), (1, 2)):
+            slots = slice(e * C, (e + 1) * C)
+            for n in range(NT):
+                nc.scalar.activation(first_relu[:, n, slots], first_sums(e, n), RELU, bias=bias_of(None, n, e))
+            nc.scalar.activation(first_square[:, 0:squared, slots], first_relu[:, 0:squared, slots], SQUARE)
+            nc.gpsimd.tensor_tensor(
+                first_gated[:, 0:squared, slots],
+                first_square[:, 0:squared, slots],
+                gate_t[:, slots].unsqueeze(1).to_broadcast([P, squared, C]),
+                MULT,
+            )
+        for n in (2, 3):
+            nc.vector.scalar_tensor_tensor(
+                first_square[:, n, C : 2 * C], first_sums(1, n), bias_of(None, n, 1), gate_t[:, C : 2 * C], ADD, MULT
+            )
+        nc.gpsimd.tensor_tensor(first_gated[:, 2:4, C : 2 * C], first_square[:, 2:4, C : 2 * C], first_relu[:, 2:4, C : 2 * C], MULT)
+        for n in (1, 3, 0, 2):
+            nc.scalar.copy(out=window[n][:, T : T + NT * E], in_=bias[:])
+        multiply(2)
+        scalar_relu(2)
+        vector_gate(2)
         multiply(3)
         scalar_relu(3, first=1, last=3)
         vector_gate(3, first=0, last=2)

@@ -71,7 +71,7 @@ def tile_moe_two_lin_relu2_kernel(tc, xT, w8_words, w8_scales, w4_words, w4_scal
         def load_scales(run, i0, i1):
             e0, e1 = GROUPS[run]
             for i in range(i0, i1):
-                a, r = divmod(i, 4)
+                r, a = divmod(i, 2)
                 nc.sync.dma_start(
                     out=w_sc[run][PLANE[a] + r : P : 32, :].bitcast(I32).rearrange("q (e n) -> q e n", e=e1 - e0),
                     in_=(w8_scales, w4_scales)[a].bitcast(I32).rearrange("e a (q r) n -> r a q e n", r=4)[r][0][:, e0:e1, :],

@@ -33,6 +33,7 @@ PIECES = tuple((m, e0, e1) for e0, e1 in ((0, 2), (2, 5), (5, 8)) for m in range
 LAST = len(PIECES) - 1
 GROUPS = ((0, 2), (2, 5), (5, 8))
 BANK = 512
+HELD = ((15, 18, 21), (18, 29), (13, 23, 28), (28, 31))
 
 
 def tile_moe_two_lin_relu2_kernel(tc, xT, w8_words, w8_scales, w4_words, w4_scales, b, gate, offs, dst, out):
@@ -50,7 +51,7 @@ def tile_moe_two_lin_relu2_kernel(tc, xT, w8_words, w8_scales, w4_words, w4_scal
         w8_t = {}
         w4_t = {}
         w_sc = [keep.tile([P, (e1 - e0) * N], U8, name=f"w_sc{e0}", align_bytes=256) for e0, e1 in GROUPS]
-        window = [keep.tile([P, T + NT * E], F32, name=f"window{n}", align_bytes=256) for n in range(NT)]
+        window = [keep.tile([P, T + E], F32, name=f"window{n}", align_bytes=256) for n in range(NT)]
         bias = keep.tile([P, NT * E], F32, name="bias")
 
         nc.gpsimd.memset(scales[:], 0)
@@ -189,7 +190,8 @@ def tile_moe_two_lin_relu2_kernel(tc, xT, w8_words, w8_scales, w4_words, w4_scal
         def bias_of(holder, n, e):
             if holder is None:
                 return bias[:, n * E + e : n * E + e + 1]
-            return window[holder][:, T + n * E + e : T + n * E + e + 1]
+            place = T + HELD[holder].index(n * E + e)
+            return window[holder][:, place : place + 1]
 
         def blocks(i, halves=(0, 1)):
             m, e0, e1 = PIECES[i]
@@ -283,7 +285,12 @@ def tile_moe_two_lin_relu2_kernel(tc, xT, w8_words, w8_scales, w4_words, w4_scal
             )
         nc.gpsimd.tensor_tensor(first_gated[:, 2:4, C : 2 * C], first_square[:, 2:4, C : 2 * C], first_relu[:, 2:4, C : 2 * C], MULT)
         for n in (1, 3, 0, 2):
-            nc.scalar.copy(out=window[n][:, T : T + NT * E], in_=bias[:])
+            for first in range(0, len(HELD[n]), 2):
+                columns = HELD[n][first : first + 2]
+                nc.scalar.copy(
+                    out=window[n][:, T + first : T + first + len(columns)],
+                    in_=bias[:, columns[0] : columns[-1] + 1 : max(columns[-1] - columns[0], 1)],
+                )
         multiply(2)
         scalar_relu(2)
         vector_gate(2)

@@ -33,7 +33,7 @@ PIECES = tuple((m, e0, e1) for e0, e1 in ((0, 2), (2, 5), (5, 8)) for m in range
 LAST = len(PIECES) - 1
 GROUPS = ((0, 2), (2, 5), (5, 8))
 BANK = 512
-HELD = ((15, 18, 21), (18, 29), (13, 23, 28), (28, 31))
+HELD = (range(15, 22, 3), range(18, 30, 11), range(13, 24, 10), range(28, 32, 3))
 
 
 def tile_moe_two_lin_relu2_kernel(tc, xT, w8_words, w8_scales, w4_words, w4_scales, b, gate, offs, dst, out):
@@ -285,18 +285,13 @@ def tile_moe_two_lin_relu2_kernel(tc, xT, w8_words, w8_scales, w4_words, w4_scal
             )
         nc.gpsimd.tensor_tensor(first_gated[:, 2:4, C : 2 * C], first_square[:, 2:4, C : 2 * C], first_relu[:, 2:4, C : 2 * C], MULT)
         for n in (1, 3, 0, 2):
-            for first in range(0, len(HELD[n]), 2):
-                columns = HELD[n][first : first + 2]
-                nc.scalar.copy(
-                    out=window[n][:, T + first : T + first + len(columns)],
-                    in_=bias[:, columns[0] : columns[-1] + 1 : max(columns[-1] - columns[0], 1)],
-                )
+            nc.scalar.copy(out=window[n][:, T : T + len(HELD[n])], in_=bias[:, HELD[n].start : HELD[n].stop : HELD[n].step])
         multiply(2)
         scalar_relu(2)
         vector_gate(2)
         multiply(3)
         scalar_relu(3, first=1, last=3)
-        vector_gate(3, first=0, last=2)
+        vector_gate(3, first=0)
         multiply(4)
         multiply(5)
         scatter(0)

import concourse.mybir as mybir
from concourse.masks import make_identity

K, T, E, C, N = 1024, 1024, 8, 128, 512
P = 128
J = 4
FLOPS = 2 * K * N * E * C
BYTES = K * T * 4 + E * 128 * 512 * 6 + 2 * E * 16 * 512 + N * E * 4 + T * 4 + 2 * P * 64 * 2 + N * T * 4

F32 = mybir.dt.float32
BF16 = mybir.dt.bfloat16
U32 = mybir.dt.uint32
I32 = mybir.dt.int32
U16 = mybir.dt.uint16
U8 = mybir.dt.uint8
FP8X4 = mybir.dt.float8_e4m3fn_x4
FP4X4 = mybir.dt.float4_e2m1fn_x4
RELU = mybir.ActivationFunctionType.Relu
COPY = mybir.ActivationFunctionType.Copy
SQUARE = mybir.ActivationFunctionType.Square
MULT = mybir.AluOpType.mult
ADD = mybir.AluOpType.add
MAX = mybir.AluOpType.max

NT = N // P
HALF = T // 2
CHUNKS = (
    ((0, 1024, 0, 2, 0), (0, 512, 2, 2, 336), (512, 512, 2, 2, 336)),
    ((0, 512, 0, 4, 0), (512, 256, 0, 4, 0), (768, 256, 0, 4, 184)),
)
PLANE = (4, 0)
PIECES = tuple((m, e0, e1) for e0, e1 in ((0, 2), (2, 5), (5, 8)) for m in range(2))
LAST = len(PIECES) - 1
GROUPS = ((0, 2), (2, 5), (5, 8))
BANK = 512
HELD = (range(15, 22, 3), range(18, 30, 11), range(13, 24, 10), range(28, 32, 3))


def tile_moe_two_lin_relu2_kernel(tc, xT, w8_words, w8_scales, w4_words, w4_scales, b, gate, offs, dst, out):
    nc = tc.nc
    with tc.tile_pool(name="keep", bufs=1) as keep, tc.psum_pool(name="psum", bufs=1) as psum:
        offs_t = keep.tile([P, 64], U16, name="offs_t")
        dst_t = keep.tile([P, 64], U16, name="dst_t")
        gate_row = keep.tile([P, E], F32, name="gate_row")
        identity = keep.tile([P, P], F32, name="identity")
        banks = [psum.tile([P, BANK], F32, name=f"bank{i}") for i in range(8)]
        words = [keep.tile([P, 2 * T if a == 0 else T], U32, name=f"words{a}", align_bytes=256) for a in range(2)]
        scales = keep.tile([P, T], U8, name="scales", align_bytes=256)
        g_words = [keep.tile([P, T], U32, name=f"g_words{a}", align_bytes=256) for a in range(2)]
        g_scales = keep.tile([P, T], U8, name="g_scales", align_bytes=256)
        w8_t = {}
        w4_t = {}
        w_sc = [keep.tile([P, (e1 - e0) * N], U8, name=f"w_sc{e0}", align_bytes=256) for e0, e1 in GROUPS]
        window = [keep.tile([P, T + E], F32, name=f"window{n}", align_bytes=256) for n in range(NT)]
        bias = keep.tile([P, NT * E], F32, name="bias")

        nc.gpsimd.memset(scales[:], 0)
        for plane_tile in w_sc:
            nc.vector.memset(plane_tile[:].bitcast(I32), 0)

        def load_words(which, e0, e1, n0, n1):
            held_in, source, size = (
                (w8_t, w8_words.rearrange("e a p n r -> (a p) e (n r)"), 4),
                (w4_t, w4_words.rearrange("e a p n -> (a p) e n"), 2),
            )[which]
            tile = keep.tile([P, e1 - e0, size * (n1 - n0)], U8, name=f"w{size}_{e0}_{n0}", align_bytes=256)
            nc.sync.dma_start(out=tile[:].bitcast(I32), in_=source[:, e0:e1, size * n0 : size * n1].bitcast(I32))
            for e in range(e0, e1):
                for n in range(n0 // P, n1 // P):
                    held_in[e, n] = tile[:, e - e0, size * (n * P - n0) : size * ((n + 1) * P - n0)]

        def load_scales(run, i0, i1):
            e0, e1 = GROUPS[run]
            for i in range(i0, i1):
                r, a = divmod(i, 2)
                nc.sync.dma_start(
                    out=w_sc[run][PLANE[a] + r : P : 32, :].bitcast(I32).rearrange("q (e n) -> q e n", e=e1 - e0),
                    in_=(w8_scales, w4_scales)[a].bitcast(I32).rearrange("e a (q r) n -> r a q e n", r=4)[r][0][:, e0:e1, :],
                )

        x_view = xT.rearrange("(a p j) t -> a p j t", a=2, j=J)
        raws = {}
        grouped = [keep.tile([P, T * J], BF16, name=f"grouped{a}", align_bytes=256) for a in range(2)]

        def load_tokens(a, i):
            t0, width, j0, rows, v = CHUNKS[a][i]
            raws[a, i] = keep.tile([P, rows, width], F32, name=f"raw{a}_{i}", tag=f"raw{a}_{i}", align_bytes=256)
            nc.sync.dma_start(out=raws[a, i][:], in_=x_view[a][:, j0 : j0 + rows, t0 : t0 + width])

        for i in range(3):
            load_tokens(0, i)
        nc.sync.dma_start(offs_t[:], offs)
        nc.sync.dma_start(out=gate_row[:], in_=gate[0].rearrange("(p j) -> p j", j=E))
        load_tokens(1, 0)
        load_scales(0, 0, 4)
        load_tokens(1, 1)
        load_tokens(1, 2)
        load_scales(0, 4, 8)
        nc.sync.dma_start(out=bias[:].rearrange("p (n e) -> p n e", e=E), in_=b.rearrange("(n p) e -> p n e", p=P))
        load_words(0, 0, 2, 0, N)
        load_words(1, 0, 2, 0, N)
        for g in (1, 2):
            e0, e1 = GROUPS[g]
            load_scales(g, 0, 3)
            load_words(0, e0, e1, 0, N // 2)
            load_scales(g, 3, 5)
            load_words(1, e0, e1, 0, N // 2)
            load_scales(g, 5, 8)
            load_words(0, e0, e1, N // 2, N)
            load_words(1, e0, e1, N // 2, N)
            if g == 1:
                nc.sync.dma_start(dst_t[:], dst)

        def round_tokens(copy, a, i, lo, hi):
            t0, width, j0, rows, v = CHUNKS[a][i]
            to = grouped[a][:, J * (t0 + lo) : J * (t0 + hi)].rearrange("p (c i j) -> p c j i", i=4, j=J)
            copy(out=to[:, :, j0 : j0 + rows, :], in_=raws[a, i][:, :, lo:hi].rearrange("p j (c i) -> p c j i", i=4))

        def interleave(a, i, cut=0):
            t0, width, j0, rows, v = CHUNKS[a][i]
            for copy, lo, hi in (
                (nc.vector.tensor_copy, 0, cut),
                (nc.vector.tensor_copy, cut, v),
                (nc.scalar.copy, v, width),
            ):
                if lo < hi:
                    round_tokens(copy, a, i, lo, hi)

        def quantise(a, t0, t1):
            nc.vector.quantize_mx(
                out=words[a][:, t0:t1].bitcast(FP8X4),
                scales=scales[PLANE[a] : P, t0:t1],
                in_=grouped[a][:, J * t0 : J * t1],
            )

        def gather(to, of, e0, e1):
            nc.vector.tensor_copy(to[:, e0 * C : e1 * C], of[:].indirect(offs_t[:, 8 * e0 : 8 * e1]))

        for t0 in (0, 512):
            round_tokens(nc.vector.tensor_copy, 0, 0, t0, t0 + 336)
            round_tokens(nc.scalar.copy, 0, 0, t0 + 336, t0 + 512)
        for h in range(2):
            interleave(0, 1 + h, cut=256)
            if h == 0:
                quantise(0, 0, 512)
        quantise(0, 512, 768)
        quantise(0, 768, 1024)
        gather(g_words[0], words[0], 0, 8)
        reused = grouped[0][:, J * 512 : J * 1024]
        nc.gpsimd.tensor_copy(
            out=reused[:, J * 256 : J * 512].rearrange("p (t j) -> p t j", j=J),
            in_=raws[1, 0][:, :, 256:512].rearrange("p j t -> p t j"),
        )
        nc.scalar.copy(
            out=reused[:, 0 : J * 256].rearrange("p (c i j) -> p c j i", i=4, j=J),
            in_=raws[1, 0][:, :, 0:256].rearrange("p j (c i) -> p c j i", i=4),
        )
        nc.vector.quantize_mx(out=words[1][:, 0:512].bitcast(FP8X4), scales=scales[:, 0:512], in_=reused)
        interleave(1, 1)
        interleave(1, 2)
        quantise(1, 512, 768)
        quantise(1, 768, 1024)
        for e0, e1 in ((0, 1), (1, 2), (2, 5), (5, 8)):
            gather(g_scales, scales, e0, e1)
            gather(g_words[1], words[1], e0, e1)

        widths = [(e1 - e0) * C for m, e0, e1 in PIECES]
        first_relu, first_square, first_gated = (
            keep.tile([P, NT, 2 * C], F32, name=f"first_{kind}") for kind in ("relu", "square", "gated")
        )
        relu = {i: keep.tile([P, 2, widths[i]], F32, name=f"relu{i}") for i in range(2, LAST + 1)}
        other = {i: keep.tile([P, 2, widths[i]], F32, name=f"other{i}") for i in range(2, LAST)}
        gated = {i: keep.tile([P, 2, widths[i]], F32, name=f"gated{i}") for i in range(2, LAST + 1)}
        result = [[first_gated[:, 2 * i + h, :] for h in range(2)] for i in range(2)]
        result = result + [[gated[i][:, h, :] for h in range(2)] for i in range(2, LAST - 1)]
        result = result + [[relu[LAST][:, 1, :], gated[LAST - 1][:, 1, :]], [other[LAST - 1][:, 0, :], gated[LAST][:, 1, :]]]

        gate_t = keep.tile([P, T], F32, name="gate_t", tag="raw1_2", align_bytes=256)
        make_identity(nc, identity[:])
        for half in range(2):
            bank = banks[6 + half]
            for j in range(J):
                column = gate_row[:, J * half + j : J * half + j + 1]
                nc.tensor.transpose(bank[:, j * P : (j + 1) * P], column.to_broadcast([P, P]), identity[:])
            nc.scalar.copy(
                out=gate_t[:].rearrange("q (p j) -> q p j", j=E)[:, :, J * half : J * (half + 1)],
                in_=bank[:].rearrange("q (j p) -> q p j", j=J),
            )

        def bias_of(holder, n, e):
            if holder is None:
                return bias[:, n * E + e : n * E + e + 1]
            place = T + HELD[holder].index(n * E + e)
            return window[holder][:, place : place + 1]

        def blocks(i, halves=(0, 1)):
            m, e0, e1 = PIECES[i]
            return [(h, 2 * m + h, e, e - e0) for h in halves for e in range(e0, e1)]

        def sums(i, h, d):
            return banks[(2 * i + 2 + h) % 8][:, d * C : (d + 1) * C]

        def first_sums(e, n):
            if e == 0:
                return banks[n][:, 0:C]
            return banks[4 + n // 2][:, (n % 2) * C : (n % 2 + 1) * C]

        def one_pass(into, a, g, e, n):
            slots = slice(e * C, (e + 1) * C)
            first = (e - GROUPS[g][0]) * N + n * P
            nc.tensor.matmul_mx(
                out=into,
                lhsT=(w8_t[e, n].bitcast(FP8X4), w4_t[e, n].bitcast(FP4X4))[a],
                lhsT_scale=w_sc[g][PLANE[a] : P, first : first + P],
                rhs=g_words[a][:, slots].bitcast(FP8X4),
                rhs_scale=g_scales[PLANE[a] : P, slots],
                start=a == 0,
                stop=a == 1,
            )

        def multiply(i):
            for h, n, e, d in blocks(i):
                for a in range(2):
                    one_pass(sums(i, h, d), a, i // 2, e, n)

        def held(steps, first, last):
            return [(step, first if k == 0 else last if k == len(steps) - 1 else None) for k, step in enumerate(steps)]

        def gate_of(i):
            m, e0, e1 = PIECES[i]
            return gate_t[:, e0 * C : e1 * C]

        def scalar_relu(i, halves=(0, 1), first=None, last=None):
            for (h, n, e, d), holder in held(blocks(i, halves), first, last):
                nc.scalar.activation(relu[i][:, h, d * C : (d + 1) * C], sums(i, h, d), RELU, bias=bias_of(holder, n, e))

        def vector_relu(i, halves, first, last):
            for (h, n, e, d), holder in held(blocks(i, halves), first, last):
                nc.vector.tensor_scalar(relu[i][:, h, d * C : (d + 1) * C], sums(i, h, d), bias_of(holder, n, e), 0.0, ADD, MAX)

        def vector_gate(i, first=None, last=None):
            for (h, n, e, d), holder in held(blocks(i), first, last):
                nc.vector.scalar_tensor_tensor(
                    other[i][:, h, d * C : (d + 1) * C],
                    sums(i, h, d),
                    bias_of(holder, n, e),
                    gate_t[:, e * C : (e + 1) * C],
                    ADD,
                    MULT,
                )
            nc.gpsimd.tensor_tensor(gated[i][:], other[i][:], relu[i][:], MULT)

        def scatter(i):
            m, e0, e1 = PIECES[i]
            places = dst_t[:, 8 * e0 : 8 * e1]
            nc.scalar.activation(window[2 * m + 1][:].indirect(places), result[i][1], COPY)
            if i == LAST:
                nc.vector.tensor_tensor(window[2 * m][:].indirect(places), result[i][0], gate_of(i), MULT)
            else:
                nc.vector.tensor_copy(window[2 * m][:].indirect(places), result[i][0])
            if e1 == E:
                for n in (2 * m + 1, 2 * m):
                    nc.sync.dma_start(out=out[n * P : (n + 1) * P, :], in_=window[n][:, 0:T])

        for a in range(2):
            for n in range(2):
                one_pass(first_sums(0, n), a, 0, 0, n)
        for e, n in ((0, 2), (0, 3), (1, 0), (1, 1), (1, 2), (1, 3)):
            for a in range(2):
                one_pass(first_sums(e, n), a, 0, e, n)
        for e, squared in ((0, NT), (1, 2)):
            slots = slice(e * C, (e + 1) * C)
            for n in range(NT):
                nc.scalar.activation(first_relu[:, n, slots], first_sums(e, n), RELU, bias=bias_of(None, n, e))
            nc.scalar.activation(first_square[:, 0:squared, slots], first_relu[:, 0:squared, slots], SQUARE)
            nc.gpsimd.tensor_tensor(
                first_gated[:, 0:squared, slots],
                first_square[:, 0:squared, slots],
                gate_t[:, slots].unsqueeze(1).to_broadcast([P, squared, C]),
                MULT,
            )
        for n in (2, 3):
            nc.vector.scalar_tensor_tensor(
                first_square[:, n, C : 2 * C], first_sums(1, n), bias_of(None, n, 1), gate_t[:, C : 2 * C], ADD, MULT
            )
        nc.gpsimd.tensor_tensor(first_gated[:, 2:4, C : 2 * C], first_square[:, 2:4, C : 2 * C], first_relu[:, 2:4, C : 2 * C], MULT)
        for n in (1, 3, 0, 2):
            nc.scalar.copy(out=window[n][:, T : T + len(HELD[n])], in_=bias[:, HELD[n].start : HELD[n].stop : HELD[n].step])
        multiply(2)
        scalar_relu(2)
        vector_gate(2)
        multiply(3)
        scalar_relu(3, first=1, last=3)
        vector_gate(3, first=0)
        multiply(4)
        multiply(5)
        scatter(0)
        vector_relu(4, (0,), None, None)
        vector_relu(4, (1,), 2, 0)
        scatter(1)
        nc.gpsimd.tensor_tensor(other[4][:], relu[4][:], relu[4][:], MULT)
        nc.gpsimd.tensor_tensor(result[4][1], other[4][:, 1, :], gate_of(4), MULT)
        scalar_relu(5, (1,), 1, 3)
        vector_relu(5, (0,), 0, 2)
        nc.gpsimd.tensor_tensor(other[4][:, 1, :], relu[5][:, 1, :], relu[5][:, 1, :], MULT)
        nc.gpsimd.tensor_tensor(result[4][0], other[4][:, 0, :], gate_of(4), MULT)
        nc.gpsimd.tensor_tensor(result[5][1], other[4][:, 1, :], gate_of(5), MULT)
        nc.gpsimd.tensor_tensor(result[5][0], relu[5][:, 0, :], relu[5][:, 0, :], MULT)
        for i in range(2, len(PIECES)):
            scatter(i)
